import numpy as np
import ml_dtypes


def mxq(x, axis, fmt="e4m3"):
    dtype, down = {"e4m3": (ml_dtypes.float8_e4m3fn, 7), "e5m2": (ml_dtypes.float8_e5m2, 14)}[fmt]
    v = np.moveaxis(np.asarray(x, np.float32).astype(ml_dtypes.bfloat16).astype(np.float64), axis, -1)
    blocks = v.reshape(v.shape[:-1] + (-1, 32))
    amax = np.abs(blocks).max(-1, keepdims=True)
    byte = np.maximum(np.where(amax > 0, np.frexp(amax)[1] - 1 + 127, 0) - down, 1)
    scale = np.exp2(byte - 127.0)
    codes = (blocks / scale).astype(np.float32).astype(dtype).astype(np.float64)
    return np.moveaxis((codes * scale).reshape(v.shape), -1, axis)


WIDE = False


def mx_kscale(k):
    if not WIDE:
        return np.ones(k)
    levels = np.array([10, -10, 5, -5, 0])
    if k % 512:
        return np.exp2(np.random.permutation(np.resize(levels, k // 32))).repeat(32)
    a = np.empty((k // 512, 16))
    for p in range(k // 512):
        a[p, :8] = np.random.permutation(np.resize(levels, 8))
        for g in range(8):
            far = levels[np.abs(levels - a[p, g]) >= 10]
            a[p, g + 8] = far[np.random.randint(len(far))]
    return np.exp2(a.ravel()).repeat(32)


def f64(x):
    return np.asarray(x).astype(np.float64)


def striped(idx):
    return np.tile(idx.reshape(-1, 16).T, (8, 1)).astype(np.uint16)


def unstriped(offs):
    return offs[:16].T.reshape(-1).astype(np.int64)


E2M1 = np.array([0.0, 0.5, 1.0, 1.5, 2.0, 3.0, 4.0, 6.0, -0.0, -0.5, -1.0, -1.5, -2.0, -3.0, -4.0, -6.0])


def pack_weight(w, fmt):
    k, n = w.shape
    w = f64(np.asarray(w, np.float32).astype(ml_dtypes.bfloat16)).reshape(k // 32, 32, n)
    amax = np.abs(w).max(1)
    if fmt == "e4m3":
        byte = np.frexp(amax)[1] - 1 + 127 - 7
    else:
        mant, ex = np.frexp(amax / 6.0)
        byte = np.where(mant > 0.5, ex, ex - 1) + 127
    byte = np.clip(np.where(amax > 0, byte, 1), 1, 254)
    scaled = (w * np.exp2(127.0 - byte)[:, None, :]).reshape(k, n).astype(np.float32)
    by_word = np.ascontiguousarray(scaled.reshape(k // 512, 128, 4, n).transpose(0, 1, 3, 2))
    if fmt == "e4m3":
        words = by_word.astype(ml_dtypes.float8_e4m3fn).view(np.uint8)
    else:
        c = by_word.astype(ml_dtypes.float4_e2m1fn).view(np.uint8) & 0xF
        words = (c[..., 0::2] | (c[..., 1::2] << 4)).reshape(k // 512, 128, 2 * n)
    return np.ascontiguousarray(words), np.ascontiguousarray(byte.astype(np.uint8).reshape(k // 512, 16, n))


def unpack_weight(words, scales, fmt):
    g, _, n = scales.shape
    words = np.ascontiguousarray(words).reshape(g, 128, n, -1)
    if fmt == "e4m3":
        vals = words.view(ml_dtypes.float8_e4m3fn).astype(np.float64)
    else:
        nib = np.empty((g, 128, n, 4), np.uint8)
        nib[..., 0::2] = words & 0xF
        nib[..., 1::2] = words >> 4
        vals = E2M1[nib]
    vals = vals * np.repeat(np.exp2(scales.astype(np.float64) - 127.0), 8, axis=1)[..., None]
    return vals.transpose(0, 1, 3, 2).reshape(g * 512, n)


def gelu(v):
    return 0.5 * v * (1.0 + np.tanh(np.sqrt(2.0 / np.pi) * (v + 0.044715 * v**3)))


K, K2, T, T2, S, H, N = 1024, 512, 2048, 4096, 1024, 1024, 512

def setup_inputs():
    n = np.random.standard_normal
    s = mx_kscale(K)[:, None]
    s2 = mx_kscale(K2)[:, None]
    u = mx_kscale(H)[:, None]
    tab_words, tab_scales = pack_weight(n((K, T)) * s, "e4m3")
    tab2_words, tab2_scales = pack_weight(n((K2, T2)) * s2, "e4m3")
    offs = striped(np.random.permutation(T)[:S])
    offs2 = striped(np.random.permutation(T2)[:S])
    w1 = (n((K, H)) / np.sqrt(K) / s * u.T).astype(np.float32)
    w2_words, w2_scales = pack_weight(n((K2, H)) / np.sqrt(K2) / s2 * u.T, "e2m1")
    b1 = (0.5 * n(H) * u[:, 0]).astype(np.float32)
    w3 = (n((H, N)) / np.sqrt(H) / u).astype(np.float32)
    b3 = (0.5 * n(N)).astype(np.float32)
    return dict(tab_words=tab_words, tab_scales=tab_scales, tab2_words=tab2_words, tab2_scales=tab2_scales,
                offs=offs, offs2=offs2, w1=w1, w2_words=w2_words, w2_scales=w2_scales, b1=b1, w3=w3, b3=b3)

def reference(tab_words, tab_scales, tab2_words, tab2_scales, offs, offs2, w1, w2_words, w2_scales, b1, w3, b3):
    v = unpack_weight(tab_words, tab_scales, "e4m3")[:, unstriped(offs)]
    v2 = unpack_weight(tab2_words, tab2_scales, "e4m3")[:, unstriped(offs2)]
    w2 = unpack_weight(w2_words, w2_scales, "e2m1")
    a = mxq(f64(w1), 0, "e4m3").T @ v
    b = w2.T @ v2
    h = np.abs(a - b + f64(b1)[:, None])
    y = mxq(f64(w3), 0, "e4m3").T @ mxq(h, 0, "e4m3")
    return np.maximum(y + f64(b3)[:, None], 0.0)

@@ -1,0 +1,242 @@
+from contextlib import ExitStack
+
+import concourse.mybir as mybir
+
+K, K2, T, T2, S, H, N = 1024, 512, 2048, 4096, 1024, 1024, 512
+FLOPS = 2 * S * (K * H + K2 * H + H * N)
+
+F32 = mybir.dt.float32
+BF16 = mybir.dt.bfloat16
+I32 = mybir.dt.int32
+U32 = mybir.dt.uint32
+U16 = mybir.dt.uint16
+U8 = mybir.dt.uint8
+FP8X4 = mybir.dt.float8_e4m3fn_x4
+FP4X4 = mybir.dt.float4_e2m1fn_x4
+ACT = mybir.ActivationFunctionType
+ALU = mybir.AluOpType
+
+P = 128
+PACK = 4
+KP = P * PACK
+NJ = 512
+V_SHARE = 88
+
+
+def tile_list_registration_pair_features_kernel(
+    tc, tab_words, tab_scales, tab2_words, tab2_scales, offs, offs2, w1, w2_words, w2_scales, b1, w3, b3, out
+):
+    nc = tc.nc
+    with ExitStack() as ctx:
+        keep = ctx.enter_context(tc.tile_pool(name="keep", bufs=1))
+        psum = ctx.enter_context(tc.psum_pool(name="psum", bufs=1))
+
+        def sb(name, shape, dtype):
+            return keep.tile(shape, dtype, name=name, align_bytes=64)
+
+        offs_sb = keep.tile([P, S // 16], U16, name="offs_sb")
+        offs2_sb = keep.tile([P, S // 16], U16, name="offs2_sb")
+        tab_w = [sb(f"tab_w{a}", [P, T], I32) for a in range(2)]
+        tab2_w = sb("tab2_w", [P, T2], I32)
+        tab_s = sb("tab_s", [P, T // 4], I32)
+        tab2_s = sb("tab2_s", [P, T2 // 4], I32)
+        w2_raw_w = sb("w2_raw_w", [P, H // 2], I32)
+        w2_raw_s = sb("w2_raw_s", [P, H // 4], I32)
+        w2_w = sb("w2_w", [P, 2 * H], U8)
+        w2_s = sb("w2_s", [P, H], U8)
+        v_w = [sb(f"v_w{a}", [P, S], U32) for a in range(2)]
+        v_s = sb("v_s", [P, S], U8)
+        v2_w = sb("v2_w", [P, S], U32)
+        v2_s = sb("v2_s", [P, S], U8)
+        w1_raw = {(b, a): sb(f"w1_raw{b}{a}", [P, PACK, KP], F32) for b in range(2) for a in range(2)}
+        w1_bf = {(b, a): sb(f"w1_bf{b}{a}", [P, KP * PACK], BF16) for b in range(2) for a in range(2)}
+        w1_w = {(b, a): sb(f"w1_w{b}{a}", [P, KP], U32) for b in range(2) for a in range(2)}
+        w1_s = {(b, a): sb(f"w1_s{b}{a}", [P, KP], U8) for b in range(2) for a in range(2)}
+        w3_raw = [sb(f"w3_raw{b}", [P, PACK, N], F32) for b in range(2)]
+        w3_bf = [sb(f"w3_bf{b}", [P, N * PACK], BF16) for b in range(2)]
+        w3_w = [sb(f"w3_w{b}", [P, N], U32) for b in range(2)]
+        w3_s = [sb(f"w3_s{b}", [P, N], U8) for b in range(2)]
+        h_rows = {(b, c): sb(f"h_rows{b}{c}", [P, PACK, NJ], BF16) for b in range(2) for c in range(2)}
+        h_bf = {(b, c): sb(f"h_bf{b}{c}", [P, NJ * PACK], BF16) for b in range(2) for c in range(2)}
+        h_w = {(b, c): sb(f"h_w{b}{c}", [P, NJ], U32) for b in range(2) for c in range(2)}
+        h_s = {(b, c): sb(f"h_s{b}{c}", [P, NJ], U8) for b in range(2) for c in range(2)}
+        b1_sb = sb("b1_sb", [P, 2, PACK], F32)
+        b3_sb = sb("b3_sb", [P, N // P], F32)
+        res = {(c, u): sb(f"res{c}{u}", [P, NJ], F32) for c in range(2) for u in range(N // P)}
+        banks = {(c, t): psum.tile([P, NJ], F32, name=f"bank{c}{t}") for c in range(2) for t in range(PACK)}
+
+        def load_w1(b, a):
+            rows = w1[KP * a : KP * (a + 1), KP * b : KP * (b + 1)]
+            nc.sync.dma_start(out=w1_raw[b, a][:], in_=rows.rearrange("(p j) c -> p j c", j=PACK))
+
+        def load_w3(b):
+            rows = w3[KP * b : KP * (b + 1), :]
+            nc.sync.dma_start(out=w3_raw[b][:], in_=rows.rearrange("(p j) c -> p j c", j=PACK))
+
+        def load_words(dst, src):
+            nc.sync.dma_start(out=dst, in_=src.rearrange("p n i -> p (n i)").bitcast(I32))
+
+        def gather(dst, window, offsets, dtype, c0, c1):
+            nc.vector.tensor_copy(
+                out=dst[:, c0:c1], in_=window[:].bitcast(dtype).indirect(offsets[:, c0 // 16 : c1 // 16])
+            )
+
+        def cast_w1(b, a, m0, m1, on_vector):
+            dst = w1_bf[b, a][:].rearrange("p (t m j) -> p m j t", t=PACK, j=PACK)[:, m0:m1]
+            src = w1_raw[b, a][:].rearrange("p j (m t) -> p m j t", t=PACK)[:, m0:m1]
+            if on_vector:
+                nc.vector.tensor_scalar(out=dst, in0=src, scalar1=-1.0, scalar2=None, op0=ALU.mult)
+            else:
+                nc.scalar.activation(out=dst, in_=src, func=ACT.Copy, scale=-1.0)
+
+        def interleave(dst, src, on_vector):
+            dst = dst[:].rearrange("p (c i t) -> p c t i", i=4, t=PACK)
+            src = src[:].rearrange("p t (c i) -> p c t i", i=4)
+            if on_vector:
+                nc.vector.tensor_copy(out=dst, in_=src)
+            else:
+                nc.scalar.copy(out=dst, in_=src)
+
+        def quantize(words, scales, src, c0, c1):
+            nc.vector.quantize_mx(
+                out=words[:, c0:c1].bitcast(FP8X4), scales=scales[:, c0:c1], in_=src[:, PACK * c0 : PACK * c1]
+            )
+
+        def mm_w2(b, c, t):
+            r0 = KP * b + P * t
+            nc.tensor.matmul_mx(
+                out=banks[c, t][:],
+                lhsT=w2_w[:, 2 * r0 : 2 * (r0 + P)].bitcast(FP4X4),
+                lhsT_scale=w2_s[:, r0 : r0 + P],
+                rhs=v2_w[:, NJ * c : NJ * (c + 1)].bitcast(FP8X4),
+                rhs_scale=v2_s[:, NJ * c : NJ * (c + 1)],
+                start=(b == 1),
+                stop=(b == 0),
+            )
+
+        def mm_w1(b, a, c, t):
+            nc.tensor.matmul_mx(
+                out=banks[c, t][:],
+                lhsT=w1_w[b, a][:, P * t : P * (t + 1)].bitcast(FP8X4),
+                lhsT_scale=w1_s[b, a][:, P * t : P * (t + 1)],
+                rhs=v_w[a][:, NJ * c : NJ * (c + 1)].bitcast(FP8X4),
+                rhs_scale=v_s[4 * (a + 1) :, NJ * c : NJ * (c + 1)],
+                start=(b == 0 and a == 0),
+                stop=(b == 1 and a == 1),
+            )
+
+        def mm_w3(b, c, u):
+            nc.tensor.matmul_mx(
+                out=banks[c, u][:],
+                lhsT=w3_w[b][:, P * u : P * (u + 1)].bitcast(FP8X4),
+                lhsT_scale=w3_s[b][:, P * u : P * (u + 1)],
+                rhs=h_w[b, c][:].bitcast(FP8X4),
+                rhs_scale=h_s[b, c][:],
+                start=(b == 0),
+                stop=(b == 1),
+            )
+
+        def evac_h(b, c, t):
+            nc.scalar.activation(
+                out=h_rows[b, c][:, t, :], in_=banks[c, t][:], func=ACT.Abs, bias=b1_sb[:, b, t : t + 1], scale=-1.0
+            )
+
+        def quantize_h(b, c):
+            quantize(h_w[b, c], h_s[b, c], h_bf[b, c], 0, NJ)
+
+        def finish(c, u, on_vector):
+            if on_vector:
+                nc.vector.tensor_scalar(
+                    out=res[c, u][:], in0=banks[c, u][:], scalar1=b3_sb[:, u : u + 1], scalar2=0.0,
+                    op0=ALU.add, op1=ALU.max,
+                )
+            else:
+                nc.scalar.activation(out=res[c, u][:], in_=banks[c, u][:], func=ACT.Relu, bias=b3_sb[:, u : u + 1])
+            nc.sync.dma_start(out=out[P * u : P * (u + 1), NJ * c : NJ * (c + 1)], in_=res[c, u][:])
+
+        nc.vector.memset(tab_s[:], 0)
+        nc.vector.memset(tab2_s[:], 0)
+        nc.vector.memset(w2_raw_s[:], 0)
+
+        nc.sync.dma_start(offs_sb[:], offs)
+        load_words(tab_w[0][:], tab_words[0])
+        nc.sync.dma_start(offs2_sb[:], offs2)
+        for q in range(4):
+            nc.gpsimd.dma_start(out=tab_s[32 * q + 4 : 32 * q + 12, :], in_=tab_scales.bitcast(I32)[:, 4 * q : 4 * q + 4, :])
+        for q in range(4):
+            nc.gpsimd.dma_start(out=tab2_s[32 * q : 32 * q + 4, :], in_=tab2_scales.bitcast(I32)[0, 4 * q : 4 * q + 4, :])
+        nc.gpsimd.dma_start(out=w2_raw_w[:], in_=w2_words[0].bitcast(I32))
+        for q in range(4):
+            nc.gpsimd.dma_start(out=w2_raw_s[32 * q : 32 * q + 4, :], in_=w2_scales.bitcast(I32)[0, 4 * q : 4 * q + 4, :])
+        load_w1(0, 0)
+        load_words(tab_w[1][:], tab_words[1])
+        load_w1(0, 1)
+        nc.sync.dma_start(out=b1_sb[:], in_=b1.rearrange("(b p t) -> p b t", b=2, t=PACK))
+        load_words(tab2_w[:], tab2_words[0])
+        load_w1(1, 0)
+        load_w1(1, 1)
+        load_w3(0)
+        load_w3(1)
+        with nc.allow_non_contiguous_dma(reason="one bias value a partition"):
+            nc.sync.dma_start(out=b3_sb[:], in_=b3.rearrange("(u p) -> p u", p=P))
+
+        gather(v_w[0], tab_w[0], offs_sb, U32, 0, S)
+        cast_w1(0, 0, 0, P, False)
+        gather(v_s, tab_s, offs_sb, U8, 0, S)
+        gather(v2_s, tab2_s, offs2_sb, U8, 0, S)
+        quantize(w1_w[0, 0], w1_s[0, 0], w1_bf[0, 0], 0, KP)
+        gather(v_w[1], tab_w[1], offs_sb, U32, 0, S)
+        cast_w1(0, 1, 0, P, False)
+        for c in range(2):
+            for t in range(PACK):
+                mm_w1(0, 0, c, t)
+        nc.vector.tensor_copy(
+            out=w2_w[:].bitcast(U16).rearrange("p (b t m) -> p b m t", b=2, t=PACK),
+            in_=w2_raw_w[:].bitcast(U16).rearrange("p (b m t) -> p b m t", b=2, t=PACK),
+        )
+        nc.vector.tensor_copy(
+            out=w2_s[:].rearrange("p (b t m) -> p b m t", b=2, t=PACK),
+            in_=w2_raw_s[:].bitcast(U8).rearrange("p (b m t) -> p b m t", b=2, t=PACK),
+        )
+        quantize(w1_w[0, 1], w1_s[0, 1], w1_bf[0, 1], 0, KP)
+        for c in range(2):
+            for t in range(PACK):
+                mm_w1(0, 1, c, t)
+        for c in range(2):
+            gather(v2_w, tab2_w, offs2_sb, U32, NJ * c, NJ * (c + 1))
+            for t in range(PACK):
+                mm_w2(0, c, t)
+                evac_h(0, c, t)
+
+        cast_w1(1, 0, 0, P, True)
+        quantize(w1_w[1, 0], w1_s[1, 0], w1_bf[1, 0], 0, KP)
+        for c in range(2):
+            for t in range(PACK):
+                mm_w2(1, c, t)
+                mm_w1(1, 0, c, t)
+        cast_w1(1, 1, 0, P, True)
+        for t in range(PACK):
+            quantize(w1_w[1, 1], w1_s[1, 1], w1_bf[1, 1], P * t, P * (t + 1))
+        for c in range(2):
+            for t in range(PACK):
+                mm_w1(1, 1, c, t)
+                evac_h(1, c, t)
+        interleave(h_bf[0, 0], h_rows[0, 0], True)
+        interleave(h_bf[0, 1], h_rows[0, 1], True)
+        quantize_h(0, 0)
+        quantize_h(0, 1)
+        interleave(w3_bf[0], w3_raw[0], True)
+        interleave(w3_bf[1], w3_raw[1], False)
+        interleave(h_bf[1, 0], h_rows[1, 0], True)
+        quantize(w3_w[0], w3_s[0], w3_bf[0], 0, N)
+        quantize_h(1, 0)
+        for c in range(2):
+            for u in range(N // P):
+                mm_w3(0, c, u)
+        interleave(h_bf[1, 1], h_rows[1, 1], True)
+        quantize(w3_w[1], w3_s[1], w3_bf[1], 0, N)
+        quantize_h(1, 1)
+        for c in range(2):
+            for u in range(N // P):
+                mm_w3(1, c, u)
+                finish(c, u, c == 1 and u % 2 == 1)

@@ -20,7 +20,7 @@ P = 128
 PACK = 4
 KP = P * PACK
 NJ = 512
-V_SHARE = 88
+OUT_CHUNKS = [(0, 512), (512, 768), (768, 1024)]
 
 
 def tile_list_registration_pair_features_kernel(
@@ -57,12 +57,12 @@ def tile_list_registration_pair_features_kernel(
         w3_w = [sb(f"w3_w{b}", [P, N], U32) for b in range(2)]
         w3_s = [sb(f"w3_s{b}", [P, N], U8) for b in range(2)]
         h_rows = {(b, c): sb(f"h_rows{b}{c}", [P, PACK, NJ], BF16) for b in range(2) for c in range(2)}
-        h_bf = {(b, c): sb(f"h_bf{b}{c}", [P, NJ * PACK], BF16) for b in range(2) for c in range(2)}
-        h_w = {(b, c): sb(f"h_w{b}{c}", [P, NJ], U32) for b in range(2) for c in range(2)}
-        h_s = {(b, c): sb(f"h_s{b}{c}", [P, NJ], U8) for b in range(2) for c in range(2)}
+        h_bf = [sb(f"h_bf{b}", [P, S * PACK], BF16) for b in range(2)]
+        h_w = [sb(f"h_w{b}", [P, S], U32) for b in range(2)]
+        h_s = [sb(f"h_s{b}", [P, S], U8) for b in range(2)]
         b1_sb = sb("b1_sb", [P, 2, PACK], F32)
         b3_sb = sb("b3_sb", [P, N // P], F32)
-        res = {(c, u): sb(f"res{c}{u}", [P, NJ], F32) for c in range(2) for u in range(N // P)}
+        res = [sb(f"res{d}", [P, N // P, c1 - c0], F32) for d, (c0, c1) in enumerate(OUT_CHUNKS)]
         banks = {(c, t): psum.tile([P, NJ], F32, name=f"bank{c}{t}") for c in range(2) for t in range(PACK)}
 
         def load_w1(b, a):
@@ -90,8 +90,8 @@ def tile_list_registration_pair_features_kernel(
                 nc.scalar.activation(out=dst, in_=src, func=ACT.Copy, scale=-1.0)
 
         def interleave(dst, src, on_vector):
-            dst = dst[:].rearrange("p (c i t) -> p c t i", i=4, t=PACK)
-            src = src[:].rearrange("p t (c i) -> p c t i", i=4)
+            dst = dst.rearrange("p (c i t) -> p c t i", i=4, t=PACK)
+            src = src.rearrange("p t (c i) -> p c t i", i=4)
             if on_vector:
                 nc.vector.tensor_copy(out=dst, in_=src)
             else:
@@ -125,13 +125,14 @@ def tile_list_registration_pair_features_kernel(
                 stop=(b == 1 and a == 1),
             )
 
-        def mm_w3(b, c, u):
+        def mm_w3(b, d, u):
+            c0, c1 = OUT_CHUNKS[d]
             nc.tensor.matmul_mx(
-                out=banks[c, u][:],
+                out=banks[d % 2, u][:, : c1 - c0],
                 lhsT=w3_w[b][:, P * u : P * (u + 1)].bitcast(FP8X4),
                 lhsT_scale=w3_s[b][:, P * u : P * (u + 1)],
-                rhs=h_w[b, c][:].bitcast(FP8X4),
-                rhs_scale=h_s[b, c][:],
+                rhs=h_w[b][:, c0:c1].bitcast(FP8X4),
+                rhs_scale=h_s[b][:, c0:c1],
                 start=(b == 0),
                 stop=(b == 1),
             )
@@ -141,35 +142,44 @@ def tile_list_registration_pair_features_kernel(
                 out=h_rows[b, c][:, t, :], in_=banks[c, t][:], func=ACT.Abs, bias=b1_sb[:, b, t : t + 1], scale=-1.0
             )
 
-        def quantize_h(b, c):
-            quantize(h_w[b, c], h_s[b, c], h_bf[b, c], 0, NJ)
+        def interleave_h(b, c0, c1):
+            c = c0 // NJ
+            interleave(h_bf[b][:, PACK * c0 : PACK * c1], h_rows[b, c][:, :, c0 - NJ * c : c1 - NJ * c], True)
 
-        def finish(c, u, on_vector):
+        def quantize_h(b, c0, c1):
+            quantize(h_w[b], h_s[b], h_bf[b], c0, c1)
+
+        def finish(d, u, on_vector):
+            c0, c1 = OUT_CHUNKS[d]
+            acc = banks[d % 2, u][:, : c1 - c0]
             if on_vector:
                 nc.vector.tensor_scalar(
-                    out=res[c, u][:], in0=banks[c, u][:], scalar1=b3_sb[:, u : u + 1], scalar2=0.0,
-                    op0=ALU.add, op1=ALU.max,
+                    out=res[d][:, u, :], in0=acc, scalar1=b3_sb[:, u : u + 1], scalar2=0.0, op0=ALU.add, op1=ALU.max
                 )
             else:
-                nc.scalar.activation(out=res[c, u][:], in_=banks[c, u][:], func=ACT.Relu, bias=b3_sb[:, u : u + 1])
-            nc.sync.dma_start(out=out[P * u : P * (u + 1), NJ * c : NJ * (c + 1)], in_=res[c, u][:])
+                nc.scalar.activation(out=res[d][:, u, :], in_=acc, func=ACT.Relu, bias=b3_sb[:, u : u + 1])
+
+        def store(d, u0, u1):
+            c0, c1 = OUT_CHUNKS[d]
+            rows = out[P * u0 : P * u1, c0:c1].rearrange("(u p) j -> p u j", p=P)
+            nc.sync.dma_start(out=rows, in_=res[d][:, u0:u1, :])
 
         nc.vector.memset(tab_s[:], 0)
-        nc.vector.memset(tab2_s[:], 0)
-        nc.vector.memset(w2_raw_s[:], 0)
+        nc.gpsimd.memset(tab2_s[:], 0)
+        nc.gpsimd.memset(w2_raw_s[:], 0)
 
         nc.sync.dma_start(offs_sb[:], offs)
+        for q in range(4):
+            nc.sync.dma_start(out=tab_s[32 * q + 4 : 32 * q + 12, :], in_=tab_scales.bitcast(I32)[:, 4 * q : 4 * q + 4, :])
         load_words(tab_w[0][:], tab_words[0])
+        load_w1(0, 0)
         nc.sync.dma_start(offs2_sb[:], offs2)
         for q in range(4):
-            nc.gpsimd.dma_start(out=tab_s[32 * q + 4 : 32 * q + 12, :], in_=tab_scales.bitcast(I32)[:, 4 * q : 4 * q + 4, :])
-        for q in range(4):
-            nc.gpsimd.dma_start(out=tab2_s[32 * q : 32 * q + 4, :], in_=tab2_scales.bitcast(I32)[0, 4 * q : 4 * q + 4, :])
-        nc.gpsimd.dma_start(out=w2_raw_w[:], in_=w2_words[0].bitcast(I32))
-        for q in range(4):
-            nc.gpsimd.dma_start(out=w2_raw_s[32 * q : 32 * q + 4, :], in_=w2_scales.bitcast(I32)[0, 4 * q : 4 * q + 4, :])
-        load_w1(0, 0)
+            nc.sync.dma_start(out=tab2_s[32 * q : 32 * q + 4, :], in_=tab2_scales.bitcast(I32)[0, 4 * q : 4 * q + 4, :])
         load_words(tab_w[1][:], tab_words[1])
+        nc.sync.dma_start(out=w2_raw_w[:], in_=w2_words[0].bitcast(I32))
+        for q in range(4):
+            nc.sync.dma_start(out=w2_raw_s[32 * q : 32 * q + 4, :], in_=w2_scales.bitcast(I32)[0, 4 * q : 4 * q + 4, :])
         load_w1(0, 1)
         nc.sync.dma_start(out=b1_sb[:], in_=b1.rearrange("(b p t) -> p b t", b=2, t=PACK))
         load_words(tab2_w[:], tab2_words[0])
@@ -180,9 +190,9 @@ def tile_list_registration_pair_features_kernel(
         with nc.allow_non_contiguous_dma(reason="one bias value a partition"):
             nc.sync.dma_start(out=b3_sb[:], in_=b3.rearrange("(u p) -> p u", p=P))
 
+        gather(v_s, tab_s, offs_sb, U8, 0, S)
         gather(v_w[0], tab_w[0], offs_sb, U32, 0, S)
         cast_w1(0, 0, 0, P, False)
-        gather(v_s, tab_s, offs_sb, U8, 0, S)
         gather(v2_s, tab2_s, offs2_sb, U8, 0, S)
         quantize(w1_w[0, 0], w1_s[0, 0], w1_bf[0, 0], 0, KP)
         gather(v_w[1], tab_w[1], offs_sb, U32, 0, S)
@@ -221,22 +231,33 @@ def tile_list_registration_pair_features_kernel(
             for t in range(PACK):
                 mm_w1(1, 1, c, t)
                 evac_h(1, c, t)
-        interleave(h_bf[0, 0], h_rows[0, 0], True)
-        interleave(h_bf[0, 1], h_rows[0, 1], True)
-        quantize_h(0, 0)
-        quantize_h(0, 1)
-        interleave(w3_bf[0], w3_raw[0], True)
-        interleave(w3_bf[1], w3_raw[1], False)
-        interleave(h_bf[1, 0], h_rows[1, 0], True)
+        interleave_h(0, 0, NJ)
+        interleave(w3_bf[0][:], w3_raw[0][:], True)
+        quantize_h(0, 0, NJ)
+        interleave_h(0, NJ, S)
         quantize(w3_w[0], w3_s[0], w3_bf[0], 0, N)
-        quantize_h(1, 0)
-        for c in range(2):
+        interleave(w3_bf[1][:], w3_raw[1][:], False)
+        interleave_h(1, 0, NJ)
+        quantize_h(0, NJ, S)
+        for d in range(2):
             for u in range(N // P):
-                mm_w3(0, c, u)
-        interleave(h_bf[1, 1], h_rows[1, 1], True)
+                mm_w3(0, d, u)
+        quantize_h(1, 0, NJ)
         quantize(w3_w[1], w3_s[1], w3_bf[1], 0, N)
-        quantize_h(1, 1)
-        for c in range(2):
-            for u in range(N // P):
-                mm_w3(1, c, u)
-                finish(c, u, c == 1 and u % 2 == 1)
+        for u in range(N // P):
+            mm_w3(1, 0, u)
+            finish(0, u, False)
+            store(0, u, u + 1)
+        interleave_h(1, 512, 768)
+        interleave_h(1, 768, 1024)
+        quantize_h(1, 512, 768)
+        quantize_h(1, 768, 1024)
+        for u in range(N // P):
+            mm_w3(1, 1, u)
+            finish(1, u, True)
+            mm_w3(0, 2, u)
+            mm_w3(1, 2, u)
+            finish(2, u, False)
+            if u % 2 == 1:
+                store(1, u - 1, u + 1)
+                store(2, u - 1, u + 1)

@@ -142,6 +142,9 @@ def tile_list_registration_pair_features_kernel(
                 out=h_rows[b, c][:, t, :], in_=banks[c, t][:], func=ACT.Abs, bias=b1_sb[:, b, t : t + 1], scale=-1.0
             )
 
+        def cast_w3(b, c0, c1, on_vector):
+            interleave(w3_bf[b][:, PACK * c0 : PACK * c1], w3_raw[b][:, :, c0:c1], on_vector)
+
         def interleave_h(b, c0, c1):
             c = c0 // NJ
             interleave(h_bf[b][:, PACK * c0 : PACK * c1], h_rows[b, c][:, :, c0 - NJ * c : c1 - NJ * c], True)
@@ -164,25 +167,27 @@ def tile_list_registration_pair_features_kernel(
             rows = out[P * u0 : P * u1, c0:c1].rearrange("(u p) j -> p u j", p=P)
             nc.sync.dma_start(out=rows, in_=res[d][:, u0:u1, :])
 
+        def load_scale_rows(dst, rows, first):
+            for r in range(4):
+                nc.sync.dma_start(out=dst[first + r : P : 32, :], in_=rows.bitcast(I32)[r : 16 : 4, :])
+
         nc.vector.memset(tab_s[:], 0)
-        nc.gpsimd.memset(tab2_s[:], 0)
+        nc.vector.memset(tab2_s[:], 0)
         nc.gpsimd.memset(w2_raw_s[:], 0)
 
         nc.sync.dma_start(offs_sb[:], offs)
-        for q in range(4):
-            nc.sync.dma_start(out=tab_s[32 * q + 4 : 32 * q + 12, :], in_=tab_scales.bitcast(I32)[:, 4 * q : 4 * q + 4, :])
         load_words(tab_w[0][:], tab_words[0])
+        load_scale_rows(tab_s, tab_scales[0], 4)
         load_w1(0, 0)
         nc.sync.dma_start(offs2_sb[:], offs2)
-        for q in range(4):
-            nc.sync.dma_start(out=tab2_s[32 * q : 32 * q + 4, :], in_=tab2_scales.bitcast(I32)[0, 4 * q : 4 * q + 4, :])
+        load_scale_rows(tab_s, tab_scales[1], 8)
         load_words(tab_w[1][:], tab_words[1])
-        nc.sync.dma_start(out=w2_raw_w[:], in_=w2_words[0].bitcast(I32))
-        for q in range(4):
-            nc.sync.dma_start(out=w2_raw_s[32 * q : 32 * q + 4, :], in_=w2_scales.bitcast(I32)[0, 4 * q : 4 * q + 4, :])
+        load_scale_rows(tab2_s, tab2_scales[0], 0)
         load_w1(0, 1)
-        nc.sync.dma_start(out=b1_sb[:], in_=b1.rearrange("(b p t) -> p b t", b=2, t=PACK))
+        nc.sync.dma_start(out=w2_raw_w[:], in_=w2_words[0].bitcast(I32))
+        load_scale_rows(w2_raw_s, w2_scales[0], 0)
         load_words(tab2_w[:], tab2_words[0])
+        nc.sync.dma_start(out=b1_sb[:], in_=b1.rearrange("(b p t) -> p b t", b=2, t=PACK))
         load_w1(1, 0)
         load_w1(1, 1)
         load_w3(0)
@@ -190,12 +195,12 @@ def tile_list_registration_pair_features_kernel(
         with nc.allow_non_contiguous_dma(reason="one bias value a partition"):
             nc.sync.dma_start(out=b3_sb[:], in_=b3.rearrange("(u p) -> p u", p=P))
 
-        gather(v_s, tab_s, offs_sb, U8, 0, S)
         gather(v_w[0], tab_w[0], offs_sb, U32, 0, S)
         cast_w1(0, 0, 0, P, False)
-        gather(v2_s, tab2_s, offs2_sb, U8, 0, S)
-        quantize(w1_w[0, 0], w1_s[0, 0], w1_bf[0, 0], 0, KP)
+        gather(v_s, tab_s, offs_sb, U8, 0, S)
         gather(v_w[1], tab_w[1], offs_sb, U32, 0, S)
+        quantize(w1_w[0, 0], w1_s[0, 0], w1_bf[0, 0], 0, KP)
+        gather(v2_s, tab2_s, offs2_sb, U8, 0, S)
         cast_w1(0, 1, 0, P, False)
         for c in range(2):
             for t in range(PACK):
@@ -220,44 +225,49 @@ def tile_list_registration_pair_features_kernel(
 
         cast_w1(1, 0, 0, P, True)
         quantize(w1_w[1, 0], w1_s[1, 0], w1_bf[1, 0], 0, KP)
-        for c in range(2):
-            for t in range(PACK):
-                mm_w2(1, c, t)
-                mm_w1(1, 0, c, t)
         cast_w1(1, 1, 0, P, True)
-        for t in range(PACK):
-            quantize(w1_w[1, 1], w1_s[1, 1], w1_bf[1, 1], P * t, P * (t + 1))
-        for c in range(2):
-            for t in range(PACK):
-                mm_w1(1, 1, c, t)
-                evac_h(1, c, t)
         interleave_h(0, 0, NJ)
-        interleave(w3_bf[0][:], w3_raw[0][:], True)
+        for t in range(0, PACK, 2):
+            quantize(w1_w[1, 1], w1_s[1, 1], w1_bf[1, 1], P * t, P * (t + 2))
+        for t in range(PACK):
+            mm_w2(1, 0, t)
+            mm_w1(1, 0, 0, t)
+        for t in range(PACK):
+            mm_w1(1, 1, 0, t)
+            evac_h(1, 0, t)
+        cast_w3(0, 0, N, True)
         quantize_h(0, 0, NJ)
-        interleave_h(0, NJ, S)
+        cast_w3(1, 0, N // 2, False)
+        cast_w3(1, N // 2, N, True)
         quantize(w3_w[0], w3_s[0], w3_bf[0], 0, N)
-        interleave(w3_bf[1][:], w3_raw[1][:], False)
+        for t in range(PACK):
+            mm_w2(1, 1, t)
+            mm_w1(1, 0, 1, t)
+            mm_w1(1, 1, 1, t)
+            evac_h(1, 1, t)
         interleave_h(1, 0, NJ)
-        quantize_h(0, NJ, S)
-        for d in range(2):
-            for u in range(N // P):
-                mm_w3(0, d, u)
-        quantize_h(1, 0, NJ)
         quantize(w3_w[1], w3_s[1], w3_bf[1], 0, N)
+        for u in range(N // P):
+            mm_w3(0, 0, u)
+        quantize_h(1, 0, NJ)
         for u in range(N // P):
             mm_w3(1, 0, u)
             finish(0, u, False)
             store(0, u, u + 1)
+        interleave_h(0, NJ, S)
         interleave_h(1, 512, 768)
-        interleave_h(1, 768, 1024)
+        quantize_h(0, NJ, S)
         quantize_h(1, 512, 768)
+        interleave_h(1, 768, 1024)
+        for u in range(N // P):
+            mm_w3(0, 1, u)
+            mm_w3(1, 1, u)
         quantize_h(1, 768, 1024)
         for u in range(N // P):
-            mm_w3(1, 1, u)
-            finish(1, u, True)
             mm_w3(0, 2, u)
             mm_w3(1, 2, u)
-            finish(2, u, False)
-            if u % 2 == 1:
-                store(1, u - 1, u + 1)
-                store(2, u - 1, u + 1)
+        for d in (1, 2):
+            for u in range(N // P):
+                finish(d, u, u >= 2)
+                if u % 2 == 1:
+                    store(d, u - 1, u + 1)

@@ -31,8 +31,8 @@ def tile_list_registration_pair_features_kernel(
         keep = ctx.enter_context(tc.tile_pool(name="keep", bufs=1))
         psum = ctx.enter_context(tc.psum_pool(name="psum", bufs=1))
 
-        def sb(name, shape, dtype):
-            return keep.tile(shape, dtype, name=name, align_bytes=64)
+        def sb(name, shape, dtype, tag=None):
+            return keep.tile(shape, dtype, name=name, tag=tag or name, align_bytes=64)
 
         offs_sb = keep.tile([P, S // 16], U16, name="offs_sb")
         offs2_sb = keep.tile([P, S // 16], U16, name="offs2_sb")
@@ -57,7 +57,7 @@ def tile_list_registration_pair_features_kernel(
         w3_w = [sb(f"w3_w{b}", [P, N], U32) for b in range(2)]
         w3_s = [sb(f"w3_s{b}", [P, N], U8) for b in range(2)]
         h_rows = {(b, c): sb(f"h_rows{b}{c}", [P, PACK, NJ], BF16) for b in range(2) for c in range(2)}
-        h_bf = [sb(f"h_bf{b}", [P, S * PACK], BF16) for b in range(2)]
+        h_bf = {}
         h_w = [sb(f"h_w{b}", [P, S], U32) for b in range(2)]
         h_s = [sb(f"h_s{b}", [P, S], U8) for b in range(2)]
         b1_sb = sb("b1_sb", [P, 2, PACK], F32)
@@ -102,7 +102,7 @@ def tile_list_registration_pair_features_kernel(
                 out=words[:, c0:c1].bitcast(FP8X4), scales=scales[:, c0:c1], in_=src[:, PACK * c0 : PACK * c1]
             )
 
-        def mm_w2(b, c, t):
+        def mm_w2(b, c, t, start, stop):
             r0 = KP * b + P * t
             nc.tensor.matmul_mx(
                 out=banks[c, t][:],
@@ -110,25 +110,30 @@ def tile_list_registration_pair_features_kernel(
                 lhsT_scale=w2_s[:, r0 : r0 + P],
                 rhs=v2_w[:, NJ * c : NJ * (c + 1)].bitcast(FP8X4),
                 rhs_scale=v2_s[:, NJ * c : NJ * (c + 1)],
-                start=(b == 1),
-                stop=(b == 0),
+                start=start,
+                stop=stop,
             )
 
-        def mm_w1(b, a, c, t):
+        def mm_w1(b, a, c, t, start, stop):
             nc.tensor.matmul_mx(
                 out=banks[c, t][:],
                 lhsT=w1_w[b, a][:, P * t : P * (t + 1)].bitcast(FP8X4),
                 lhsT_scale=w1_s[b, a][:, P * t : P * (t + 1)],
                 rhs=v_w[a][:, NJ * c : NJ * (c + 1)].bitcast(FP8X4),
                 rhs_scale=v_s[4 * (a + 1) :, NJ * c : NJ * (c + 1)],
-                start=(b == 0 and a == 0),
-                stop=(b == 1 and a == 1),
+                start=start,
+                stop=stop,
             )
+
+        def out_acc(d, u):
+            if d == 0:
+                return banks[0, u][:]
+            return banks[1, 2 * (d - 1) + u // 2][:, 256 * (u % 2) : 256 * (u % 2 + 1)]
 
         def mm_w3(b, d, u):
             c0, c1 = OUT_CHUNKS[d]
             nc.tensor.matmul_mx(
-                out=banks[d % 2, u][:, : c1 - c0],
+                out=out_acc(d, u),
                 lhsT=w3_w[b][:, P * u : P * (u + 1)].bitcast(FP8X4),
                 lhsT_scale=w3_s[b][:, P * u : P * (u + 1)],
                 rhs=h_w[b][:, c0:c1].bitcast(FP8X4),
@@ -137,9 +142,13 @@ def tile_list_registration_pair_features_kernel(
                 stop=(b == 1),
             )
 
-        def evac_h(b, c, t):
+        def evac_h(b, c, t, j0=0, j1=NJ):
             nc.scalar.activation(
-                out=h_rows[b, c][:, t, :], in_=banks[c, t][:], func=ACT.Abs, bias=b1_sb[:, b, t : t + 1], scale=-1.0
+                out=h_rows[b, c][:, t, j0:j1],
+                in_=banks[c, t][:, j0:j1],
+                func=ACT.Abs,
+                bias=b1_sb[:, b, t : t + 1],
+                scale=-1.0,
             )
 
         def cast_w3(b, c0, c1, on_vector):
@@ -147,14 +156,20 @@ def tile_list_registration_pair_features_kernel(
 
         def interleave_h(b, c0, c1):
             c = c0 // NJ
-            interleave(h_bf[b][:, PACK * c0 : PACK * c1], h_rows[b, c][:, :, c0 - NJ * c : c1 - NJ * c], True)
+            j0, j1 = c0 - NJ * c, c1 - NJ * c
+            interleave(h_bf[b, c][:, PACK * j0 : PACK * j1], h_rows[b, c][:, :, j0:j1], True)
 
         def quantize_h(b, c0, c1):
-            quantize(h_w[b], h_s[b], h_bf[b], c0, c1)
+            c = c0 // NJ
+            nc.vector.quantize_mx(
+                out=h_w[b][:, c0:c1].bitcast(FP8X4),
+                scales=h_s[b][:, c0:c1],
+                in_=h_bf[b, c][:, PACK * (c0 - NJ * c) : PACK * (c1 - NJ * c)],
+            )
 
         def finish(d, u, on_vector):
             c0, c1 = OUT_CHUNKS[d]
-            acc = banks[d % 2, u][:, : c1 - c0]
+            acc = out_acc(d, u)
             if on_vector:
                 nc.vector.tensor_scalar(
                     out=res[d][:, u, :], in0=acc, scalar1=b3_sb[:, u : u + 1], scalar2=0.0, op0=ALU.add, op1=ALU.max
@@ -171,23 +186,23 @@ def tile_list_registration_pair_features_kernel(
             for r in range(4):
                 nc.sync.dma_start(out=dst[first + r : P : 32, :], in_=rows.bitcast(I32)[r : 16 : 4, :])
 
+        nc.gpsimd.memset(tab2_s[:], 0)
         nc.vector.memset(tab_s[:], 0)
-        nc.vector.memset(tab2_s[:], 0)
-        nc.gpsimd.memset(w2_raw_s[:], 0)
+        nc.vector.memset(w2_raw_s[:], 0)
 
+        nc.sync.dma_start(out=w2_raw_w[:], in_=w2_words[0].bitcast(I32))
+        nc.sync.dma_start(offs2_sb[:], offs2)
         nc.sync.dma_start(offs_sb[:], offs)
+        load_scale_rows(tab2_s, tab2_scales[0], 0)
         load_words(tab_w[0][:], tab_words[0])
         load_scale_rows(tab_s, tab_scales[0], 4)
         load_w1(0, 0)
-        nc.sync.dma_start(offs2_sb[:], offs2)
         load_scale_rows(tab_s, tab_scales[1], 8)
         load_words(tab_w[1][:], tab_words[1])
-        load_scale_rows(tab2_s, tab2_scales[0], 0)
-        load_w1(0, 1)
-        nc.sync.dma_start(out=w2_raw_w[:], in_=w2_words[0].bitcast(I32))
         load_scale_rows(w2_raw_s, w2_scales[0], 0)
         load_words(tab2_w[:], tab2_words[0])
         nc.sync.dma_start(out=b1_sb[:], in_=b1.rearrange("(b p t) -> p b t", b=2, t=PACK))
+        load_w1(0, 1)
         load_w1(1, 0)
         load_w1(1, 1)
         load_w3(0)
@@ -195,65 +210,72 @@ def tile_list_registration_pair_features_kernel(
         with nc.allow_non_contiguous_dma(reason="one bias value a partition"):
             nc.sync.dma_start(out=b3_sb[:], in_=b3.rearrange("(u p) -> p u", p=P))
 
-        gather(v_w[0], tab_w[0], offs_sb, U32, 0, S)
-        cast_w1(0, 0, 0, P, False)
-        gather(v_s, tab_s, offs_sb, U8, 0, S)
-        gather(v_w[1], tab_w[1], offs_sb, U32, 0, S)
-        quantize(w1_w[0, 0], w1_s[0, 0], w1_bf[0, 0], 0, KP)
-        gather(v2_s, tab2_s, offs2_sb, U8, 0, S)
-        cast_w1(0, 1, 0, P, False)
-        for c in range(2):
-            for t in range(PACK):
-                mm_w1(0, 0, c, t)
         nc.vector.tensor_copy(
             out=w2_w[:].bitcast(U16).rearrange("p (b t m) -> p b m t", b=2, t=PACK),
             in_=w2_raw_w[:].bitcast(U16).rearrange("p (b m t) -> p b m t", b=2, t=PACK),
         )
+        gather(v2_s, tab2_s, offs2_sb, U8, 0, S)
+        gather(v_w[0], tab_w[0], offs_sb, U32, 0, S)
+        cast_w1(0, 0, 0, P, False)
+        gather(v_s, tab_s, offs_sb, U8, 0, S)
+        quantize(w1_w[0, 0], w1_s[0, 0], w1_bf[0, 0], 0, KP)
+        gather(v_w[1], tab_w[1], offs_sb, U32, 0, S)
+        for c in range(2):
+            for t in range(PACK):
+                mm_w1(0, 0, c, t, True, False)
         nc.vector.tensor_copy(
             out=w2_s[:].rearrange("p (b t m) -> p b m t", b=2, t=PACK),
             in_=w2_raw_s[:].bitcast(U8).rearrange("p (b m t) -> p b m t", b=2, t=PACK),
         )
-        quantize(w1_w[0, 1], w1_s[0, 1], w1_bf[0, 1], 0, KP)
-        for c in range(2):
-            for t in range(PACK):
-                mm_w1(0, 1, c, t)
         for c in range(2):
             gather(v2_w, tab2_w, offs2_sb, U32, NJ * c, NJ * (c + 1))
             for t in range(PACK):
-                mm_w2(0, c, t)
+                mm_w2(0, c, t, False, False)
+        cast_w1(0, 1, 0, 44, False)
+        cast_w1(0, 1, 44, P, True)
+        for t in range(0, PACK, 2):
+            quantize(w1_w[0, 1], w1_s[0, 1], w1_bf[0, 1], P * t, P * (t + 2))
+        for c in range(2):
+            for t in range(PACK):
+                mm_w1(0, 1, c, t, False, True)
                 evac_h(0, c, t)
 
         cast_w1(1, 0, 0, P, True)
         quantize(w1_w[1, 0], w1_s[1, 0], w1_bf[1, 0], 0, KP)
         cast_w1(1, 1, 0, P, True)
-        interleave_h(0, 0, NJ)
         for t in range(0, PACK, 2):
             quantize(w1_w[1, 1], w1_s[1, 1], w1_bf[1, 1], P * t, P * (t + 2))
-        for t in range(PACK):
-            mm_w2(1, 0, t)
-            mm_w1(1, 0, 0, t)
-        for t in range(PACK):
-            mm_w1(1, 1, 0, t)
-            evac_h(1, 0, t)
-        cast_w3(0, 0, N, True)
+        h_bf[0, 0] = sb("h_bf00", [P, NJ * PACK], BF16, tag="w1_raw11")
+        interleave_h(0, 0, NJ)
         quantize_h(0, 0, NJ)
+        for t in range(PACK):
+            mm_w2(1, 0, t, True, False)
+            mm_w1(1, 0, 0, t, False, False)
+        for t in range(PACK):
+            mm_w1(1, 1, 0, t, False, True)
+            evac_h(1, 0, t)
+        for t in range(PACK):
+            mm_w1(1, 1, 1, t, True, False)
+            mm_w1(1, 0, 1, t, False, False)
+            mm_w2(1, 1, t, False, True)
+        cast_w3(0, 0, N, True)
         cast_w3(1, 0, N // 2, False)
         cast_w3(1, N // 2, N, True)
-        quantize(w3_w[0], w3_s[0], w3_bf[0], 0, N)
-        for t in range(PACK):
-            mm_w2(1, 1, t)
-            mm_w1(1, 0, 1, t)
-            mm_w1(1, 1, 1, t)
-            evac_h(1, 1, t)
+        h_bf[1, 0] = sb("h_bf10", [P, NJ * PACK], BF16)
         interleave_h(1, 0, NJ)
+        quantize(w3_w[0], w3_s[0], w3_bf[0], 0, N)
         quantize(w3_w[1], w3_s[1], w3_bf[1], 0, N)
+        quantize_h(1, 0, NJ)
+        for j0 in (0, NJ // 2):
+            for t in range(PACK):
+                evac_h(1, 1, t, j0, j0 + NJ // 2)
         for u in range(N // P):
             mm_w3(0, 0, u)
-        quantize_h(1, 0, NJ)
-        for u in range(N // P):
             mm_w3(1, 0, u)
             finish(0, u, False)
             store(0, u, u + 1)
+        h_bf[0, 1] = sb("h_bf01", [P, NJ * PACK], BF16, tag="h_bf10")
+        h_bf[1, 1] = sb("h_bf11", [P, NJ * PACK], BF16)
         interleave_h(0, NJ, S)
         interleave_h(1, 512, 768)
         quantize_h(0, NJ, S)
@@ -268,6 +290,6 @@ def tile_list_registration_pair_features_kernel(
             mm_w3(1, 2, u)
         for d in (1, 2):
             for u in range(N // P):
-                finish(d, u, u >= 2)
+                finish(d, u, d == 2 and u >= 2)
                 if u % 2 == 1:
                     store(d, u - 1, u + 1)

@@ -45,9 +45,11 @@ def tile_list_registration_pair_features_kernel(
         w2_w = sb("w2_w", [P, 2 * H], U8)
         w2_s = sb("w2_s", [P, H], U8)
         v_w = [sb(f"v_w{a}", [P, S], U32) for a in range(2)]
-        v_s = sb("v_s", [P, S], U8)
+        v_s = [sb(f"v_s{a}", [P, S], U8) for a in range(2)]
         v2_w = sb("v2_w", [P, S], U32)
         v2_s = sb("v2_s", [P, S], U8)
+        v_rows = sb("v_rows", [P, S], U8)
+        v2_rows = sb("v2_rows", [P, S], U8)
         w1_raw = {(b, a): sb(f"w1_raw{b}{a}", [P, PACK, KP], F32) for b in range(2) for a in range(2)}
         w1_bf = {(b, a): sb(f"w1_bf{b}{a}", [P, KP * PACK], BF16) for b in range(2) for a in range(2)}
         w1_w = {(b, a): sb(f"w1_w{b}{a}", [P, KP], U32) for b in range(2) for a in range(2)}
@@ -120,7 +122,7 @@ def tile_list_registration_pair_features_kernel(
                 lhsT=w1_w[b, a][:, P * t : P * (t + 1)].bitcast(FP8X4),
                 lhsT_scale=w1_s[b, a][:, P * t : P * (t + 1)],
                 rhs=v_w[a][:, NJ * c : NJ * (c + 1)].bitcast(FP8X4),
-                rhs_scale=v_s[4 * (a + 1) :, NJ * c : NJ * (c + 1)],
+                rhs_scale=v_s[a][4 * (a + 1) :, NJ * c : NJ * (c + 1)],
                 start=start,
                 stop=stop,
             )
@@ -186,23 +188,42 @@ def tile_list_registration_pair_features_kernel(
             for r in range(4):
                 nc.sync.dma_start(out=dst[first + r : P : 32, :], in_=rows.bitcast(I32)[r : 16 : 4, :])
 
-        nc.gpsimd.memset(tab2_s[:], 0)
-        nc.vector.memset(tab_s[:], 0)
-        nc.vector.memset(w2_raw_s[:], 0)
+        def move_scale_rows(dst, first, src, src_first, src_step):
+            for r in range(4):
+                p0 = src_first + src_step * r
+                nc.sync.dma_start(
+                    out=dst[:].bitcast(I32)[first + r : P : 32, :],
+                    in_=src[:].bitcast(I32)[p0 : p0 + 12 * src_step + 1 : 4 * src_step, :],
+                )
+
+        nc.gpsimd.memset(tab_s[:], 0)
+        nc.vector.memset(tab2_s[:], 0)
+        nc.gpsimd.memset(w2_raw_s[:], 0)
+        for a in range(2):
+            nc.vector.memset(v_s[a][:].bitcast(I32), 0)
+        nc.vector.memset(v2_s[:].bitcast(I32), 0)
 
         nc.sync.dma_start(out=w2_raw_w[:], in_=w2_words[0].bitcast(I32))
-        nc.sync.dma_start(offs2_sb[:], offs2)
         nc.sync.dma_start(offs_sb[:], offs)
-        load_scale_rows(tab2_s, tab2_scales[0], 0)
+        nc.sync.dma_start(out=tab_s[0:P:4, :], in_=tab_scales.rearrange("a q t -> (a q) t").bitcast(I32))
+        nc.sync.dma_start(offs2_sb[:], offs2)
+        nc.sync.dma_start(out=tab2_s[0:P:8, :], in_=tab2_scales[0].bitcast(I32))
         load_words(tab_w[0][:], tab_words[0])
-        load_scale_rows(tab_s, tab_scales[0], 4)
-        load_w1(0, 0)
-        load_scale_rows(tab_s, tab_scales[1], 8)
-        load_words(tab_w[1][:], tab_words[1])
         load_scale_rows(w2_raw_s, w2_scales[0], 0)
+        load_w1(0, 0)
+        load_words(tab_w[1][:], tab_words[1])
+        nc.vector.tensor_copy(
+            out=w2_w[:].bitcast(U16).rearrange("p (b t m) -> p b m t", b=2, t=PACK),
+            in_=w2_raw_w[:].bitcast(U16).rearrange("p (b m t) -> p b m t", b=2, t=PACK),
+        )
+        gather(v_rows, tab_s, offs_sb, U8, 0, S)
+        gather(v2_rows, tab2_s, offs2_sb, U8, 0, S)
+        move_scale_rows(v_s[0], 4, v_rows, 0, 4)
         load_words(tab2_w[:], tab2_words[0])
-        nc.sync.dma_start(out=b1_sb[:], in_=b1.rearrange("(b p t) -> p b t", b=2, t=PACK))
+        move_scale_rows(v2_s, 0, v2_rows, 0, 8)
         load_w1(0, 1)
+        move_scale_rows(v_s[1], 8, v_rows, 64, 4)
+        nc.sync.dma_start(out=b1_sb[:], in_=b1.rearrange("(b p t) -> p b t", b=2, t=PACK))
         load_w1(1, 0)
         load_w1(1, 1)
         load_w3(0)
@@ -210,14 +231,8 @@ def tile_list_registration_pair_features_kernel(
         with nc.allow_non_contiguous_dma(reason="one bias value a partition"):
             nc.sync.dma_start(out=b3_sb[:], in_=b3.rearrange("(u p) -> p u", p=P))
 
-        nc.vector.tensor_copy(
-            out=w2_w[:].bitcast(U16).rearrange("p (b t m) -> p b m t", b=2, t=PACK),
-            in_=w2_raw_w[:].bitcast(U16).rearrange("p (b m t) -> p b m t", b=2, t=PACK),
-        )
-        gather(v2_s, tab2_s, offs2_sb, U8, 0, S)
         gather(v_w[0], tab_w[0], offs_sb, U32, 0, S)
         cast_w1(0, 0, 0, P, False)
-        gather(v_s, tab_s, offs_sb, U8, 0, S)
         quantize(w1_w[0, 0], w1_s[0, 0], w1_bf[0, 0], 0, KP)
         gather(v_w[1], tab_w[1], offs_sb, U32, 0, S)
         for c in range(2):

@@ -60,6 +60,7 @@ def tile_list_registration_pair_features_kernel(
         w3_s = [sb(f"w3_s{b}", [P, N], U8) for b in range(2)]
         h_rows = {(b, c): sb(f"h_rows{b}{c}", [P, PACK, NJ], BF16) for b in range(2) for c in range(2)}
         h_bf = {}
+        HALF = NJ // 2
         h_w = [sb(f"h_w{b}", [P, S], U32) for b in range(2)]
         h_s = [sb(f"h_s{b}", [P, S], U8) for b in range(2)]
         b1_sb = sb("b1_sb", [P, 2, PACK], F32)
@@ -128,9 +129,8 @@ def tile_list_registration_pair_features_kernel(
             )
 
         def out_acc(d, u):
-            if d == 0:
-                return banks[0, u][:]
-            return banks[1, 2 * (d - 1) + u // 2][:, 256 * (u % 2) : 256 * (u % 2 + 1)]
+            c0, c1 = OUT_CHUNKS[d]
+            return banks[d % 2, u][:, : c1 - c0]
 
         def mm_w3(b, d, u):
             c0, c1 = OUT_CHUNKS[d]
@@ -156,18 +156,17 @@ def tile_list_registration_pair_features_kernel(
         def cast_w3(b, c0, c1, on_vector):
             interleave(w3_bf[b][:, PACK * c0 : PACK * c1], w3_raw[b][:, :, c0:c1], on_vector)
 
-        def interleave_h(b, c0, c1):
+        def interleave_h(b, c0, c1, tag=None):
             c = c0 // NJ
-            j0, j1 = c0 - NJ * c, c1 - NJ * c
-            interleave(h_bf[b, c][:, PACK * j0 : PACK * j1], h_rows[b, c][:, :, j0:j1], True)
+            h_bf[b, c0] = sb(f"h_bf{b}_{c0}", [P, (c1 - c0) * PACK], BF16, tag=tag)
+            interleave(h_bf[b, c0][:], h_rows[b, c][:, :, c0 - NJ * c : c1 - NJ * c], True)
+
+        def h_src(b, c0, c1):
+            first = max(f for bb, f in h_bf if bb == b and f <= c0)
+            return h_bf[b, first][:, PACK * (c0 - first) : PACK * (c1 - first)]
 
         def quantize_h(b, c0, c1):
-            c = c0 // NJ
-            nc.vector.quantize_mx(
-                out=h_w[b][:, c0:c1].bitcast(FP8X4),
-                scales=h_s[b][:, c0:c1],
-                in_=h_bf[b, c][:, PACK * (c0 - NJ * c) : PACK * (c1 - NJ * c)],
-            )
+            nc.vector.quantize_mx(out=h_w[b][:, c0:c1].bitcast(FP8X4), scales=h_s[b][:, c0:c1], in_=h_src(b, c0, c1))
 
         def finish(d, u, on_vector):
             c0, c1 = OUT_CHUNKS[d]
@@ -253,16 +252,21 @@ def tile_list_registration_pair_features_kernel(
         for c in range(2):
             for t in range(PACK):
                 mm_w1(0, 1, c, t, False, True)
-                evac_h(0, c, t)
+        for j0 in (0, HALF):
+            for t in range(PACK):
+                evac_h(0, 0, t, j0, j0 + HALF)
+        for t in range(PACK):
+            evac_h(0, 1, t)
 
         cast_w1(1, 0, 0, P, True)
         quantize(w1_w[1, 0], w1_s[1, 0], w1_bf[1, 0], 0, KP)
+        interleave_h(0, 0, HALF, tag="w1_raw10")
+        quantize_h(0, 0, HALF)
         cast_w1(1, 1, 0, P, True)
         for t in range(0, PACK, 2):
             quantize(w1_w[1, 1], w1_s[1, 1], w1_bf[1, 1], P * t, P * (t + 2))
-        h_bf[0, 0] = sb("h_bf00", [P, NJ * PACK], BF16, tag="w1_raw11")
-        interleave_h(0, 0, NJ)
-        quantize_h(0, 0, NJ)
+        interleave_h(0, HALF, NJ, tag="w1_raw11")
+        quantize_h(0, HALF, NJ)
         for t in range(PACK):
             mm_w2(1, 0, t, True, False)
             mm_w1(1, 0, 0, t, False, False)
@@ -276,35 +280,30 @@ def tile_list_registration_pair_features_kernel(
         cast_w3(0, 0, N, True)
         cast_w3(1, 0, N // 2, False)
         cast_w3(1, N // 2, N, True)
-        h_bf[1, 0] = sb("h_bf10", [P, NJ * PACK], BF16)
         interleave_h(1, 0, NJ)
         quantize(w3_w[0], w3_s[0], w3_bf[0], 0, N)
         quantize(w3_w[1], w3_s[1], w3_bf[1], 0, N)
+        interleave_h(0, NJ, S, tag="w3_raw1")
         quantize_h(1, 0, NJ)
-        for j0 in (0, NJ // 2):
-            for t in range(PACK):
-                evac_h(1, 1, t, j0, j0 + NJ // 2)
+        for t in range(PACK):
+            evac_h(1, 1, t)
         for u in range(N // P):
             mm_w3(0, 0, u)
+        for u in range(N // P):
             mm_w3(1, 0, u)
             finish(0, u, False)
             store(0, u, u + 1)
-        h_bf[0, 1] = sb("h_bf01", [P, NJ * PACK], BF16, tag="h_bf10")
-        h_bf[1, 1] = sb("h_bf11", [P, NJ * PACK], BF16)
-        interleave_h(0, NJ, S)
-        interleave_h(1, 512, 768)
         quantize_h(0, NJ, S)
-        quantize_h(1, 512, 768)
+        interleave_h(1, 512, 768)
         interleave_h(1, 768, 1024)
-        for u in range(N // P):
-            mm_w3(0, 1, u)
-            mm_w3(1, 1, u)
+        quantize_h(1, 512, 768)
         quantize_h(1, 768, 1024)
-        for u in range(N // P):
-            mm_w3(0, 2, u)
-            mm_w3(1, 2, u)
+        for d in (1, 2):
+            for b in range(2):
+                for u in range(N // P):
+                    mm_w3(b, d, u)
         for d in (1, 2):
             for u in range(N // P):
-                finish(d, u, d == 2 and u >= 2)
+                finish(d, u, u % 2 == 1)
                 if u % 2 == 1:
                     store(d, u - 1, u + 1)

@@ -84,9 +84,9 @@ def tile_list_registration_pair_features_kernel(
                 out=dst[:, c0:c1], in_=window[:].bitcast(dtype).indirect(offsets[:, c0 // 16 : c1 // 16])
             )
 
-        def cast_w1(b, a, m0, m1, on_vector):
-            dst = w1_bf[b, a][:].rearrange("p (t m j) -> p m j t", t=PACK, j=PACK)[:, m0:m1]
-            src = w1_raw[b, a][:].rearrange("p j (m t) -> p m j t", t=PACK)[:, m0:m1]
+        def cast_w1(b, a, t0, t1, on_vector):
+            dst = w1_bf[b, a][:].rearrange("p (t m j) -> p m j t", t=PACK, j=PACK)[:, :, :, t0:t1]
+            src = w1_raw[b, a][:].rearrange("p j (m t) -> p m j t", t=PACK)[:, :, :, t0:t1]
             if on_vector:
                 nc.vector.tensor_scalar(out=dst, in0=src, scalar1=-1.0, scalar2=None, op0=ALU.mult)
             else:
@@ -205,11 +205,11 @@ def tile_list_registration_pair_features_kernel(
         nc.sync.dma_start(out=w2_raw_w[:], in_=w2_words[0].bitcast(I32))
         nc.sync.dma_start(offs_sb[:], offs)
         nc.sync.dma_start(out=tab_s[0:P:4, :], in_=tab_scales.rearrange("a q t -> (a q) t").bitcast(I32))
+        load_words(tab_w[0][:], tab_words[0])
         nc.sync.dma_start(offs2_sb[:], offs2)
         nc.sync.dma_start(out=tab2_s[0:P:8, :], in_=tab2_scales[0].bitcast(I32))
-        load_words(tab_w[0][:], tab_words[0])
-        load_scale_rows(w2_raw_s, w2_scales[0], 0)
         load_w1(0, 0)
+        load_scale_rows(w2_raw_s, w2_scales[0], 0)
         load_words(tab_w[1][:], tab_words[1])
         nc.vector.tensor_copy(
             out=w2_w[:].bitcast(U16).rearrange("p (b t m) -> p b m t", b=2, t=PACK),
@@ -231,7 +231,7 @@ def tile_list_registration_pair_features_kernel(
             nc.sync.dma_start(out=b3_sb[:], in_=b3.rearrange("(u p) -> p u", p=P))
 
         gather(v_w[0], tab_w[0], offs_sb, U32, 0, S)
-        cast_w1(0, 0, 0, P, False)
+        cast_w1(0, 0, 0, PACK, False)
         quantize(w1_w[0, 0], w1_s[0, 0], w1_bf[0, 0], 0, KP)
         gather(v_w[1], tab_w[1], offs_sb, U32, 0, S)
         for c in range(2):
@@ -245,8 +245,8 @@ def tile_list_registration_pair_features_kernel(
             gather(v2_w, tab2_w, offs2_sb, U32, NJ * c, NJ * (c + 1))
             for t in range(PACK):
                 mm_w2(0, c, t, False, False)
-        cast_w1(0, 1, 0, 44, False)
-        cast_w1(0, 1, 44, P, True)
+        cast_w1(0, 1, 0, 2, True)
+        cast_w1(0, 1, 2, PACK, False)
         for t in range(0, PACK, 2):
             quantize(w1_w[0, 1], w1_s[0, 1], w1_bf[0, 1], P * t, P * (t + 2))
         for c in range(2):
@@ -258,11 +258,11 @@ def tile_list_registration_pair_features_kernel(
         for t in range(PACK):
             evac_h(0, 1, t)
 
-        cast_w1(1, 0, 0, P, True)
+        cast_w1(1, 0, 0, PACK, True)
         quantize(w1_w[1, 0], w1_s[1, 0], w1_bf[1, 0], 0, KP)
         interleave_h(0, 0, HALF, tag="w1_raw10")
         quantize_h(0, 0, HALF)
-        cast_w1(1, 1, 0, P, True)
+        cast_w1(1, 1, 0, PACK, True)
         for t in range(0, PACK, 2):
             quantize(w1_w[1, 1], w1_s[1, 1], w1_bf[1, 1], P * t, P * (t + 2))
         interleave_h(0, HALF, NJ, tag="w1_raw11")
@@ -283,20 +283,22 @@ def tile_list_registration_pair_features_kernel(
         interleave_h(1, 0, NJ)
         quantize(w3_w[0], w3_s[0], w3_bf[0], 0, N)
         quantize(w3_w[1], w3_s[1], w3_bf[1], 0, N)
-        interleave_h(0, NJ, S, tag="w3_raw1")
         quantize_h(1, 0, NJ)
+        interleave_h(0, 512, 768, tag="h_bf1_0")
         for t in range(PACK):
             evac_h(1, 1, t)
         for u in range(N // P):
             mm_w3(0, 0, u)
         for u in range(N // P):
             mm_w3(1, 0, u)
-            finish(0, u, False)
+            finish(0, u, u == 0)
             store(0, u, u + 1)
-        quantize_h(0, NJ, S)
         interleave_h(1, 512, 768)
-        interleave_h(1, 768, 1024)
+        quantize_h(0, 512, 768)
+        interleave_h(0, 768, 1024, tag="h_bf1_0")
         quantize_h(1, 512, 768)
+        interleave_h(1, 768, 1024)
+        quantize_h(0, 768, 1024)
         quantize_h(1, 768, 1024)
         for d in (1, 2):
             for b in range(2):
@@ -304,6 +306,6 @@ def tile_list_registration_pair_features_kernel(
                     mm_w3(b, d, u)
         for d in (1, 2):
             for u in range(N // P):
-                finish(d, u, u % 2 == 1)
+                finish(d, u, d == 2 and u % 2 == 1)
                 if u % 2 == 1:
                     store(d, u - 1, u + 1)

@@ -51,7 +51,7 @@ def tile_list_registration_pair_features_kernel(
         v_rows = sb("v_rows", [P, S], U8)
         v2_rows = sb("v2_rows", [P, S], U8)
         w1_raw = {(b, a): sb(f"w1_raw{b}{a}", [P, PACK, KP], F32) for b in range(2) for a in range(2)}
-        w1_bf = {(b, a): sb(f"w1_bf{b}{a}", [P, KP * PACK], BF16) for b in range(2) for a in range(2)}
+        w1_bf = {}
         w1_w = {(b, a): sb(f"w1_w{b}{a}", [P, KP], U32) for b in range(2) for a in range(2)}
         w1_s = {(b, a): sb(f"w1_s{b}{a}", [P, KP], U8) for b in range(2) for a in range(2)}
         w3_raw = [sb(f"w3_raw{b}", [P, PACK, N], F32) for b in range(2)]
@@ -85,7 +85,8 @@ def tile_list_registration_pair_features_kernel(
             )
 
         def cast_w1(b, a, t0, t1, on_vector):
-            dst = w1_bf[b, a][:].rearrange("p (t m j) -> p m j t", t=PACK, j=PACK)[:, :, :, t0:t1]
+            w1_bf[b, a, t0] = sb(f"w1_bf{b}{a}{t0}", [P, (t1 - t0) * KP], BF16)
+            dst = w1_bf[b, a, t0][:].rearrange("p (t m j) -> p m j t", t=t1 - t0, j=PACK)
             src = w1_raw[b, a][:].rearrange("p j (m t) -> p m j t", t=PACK)[:, :, :, t0:t1]
             if on_vector:
                 nc.vector.tensor_scalar(out=dst, in0=src, scalar1=-1.0, scalar2=None, op0=ALU.mult)
@@ -103,6 +104,13 @@ def tile_list_registration_pair_features_kernel(
         def quantize(words, scales, src, c0, c1):
             nc.vector.quantize_mx(
                 out=words[:, c0:c1].bitcast(FP8X4), scales=scales[:, c0:c1], in_=src[:, PACK * c0 : PACK * c1]
+            )
+
+        def quantize_w1(b, a, t0, t1):
+            nc.vector.quantize_mx(
+                out=w1_w[b, a][:, P * t0 : P * t1].bitcast(FP8X4),
+                scales=w1_s[b, a][:, P * t0 : P * t1],
+                in_=w1_bf[b, a, t0][:],
             )
 
         def mm_w2(b, c, t, start, stop):
@@ -232,7 +240,7 @@ def tile_list_registration_pair_features_kernel(
 
         gather(v_w[0], tab_w[0], offs_sb, U32, 0, S)
         cast_w1(0, 0, 0, PACK, False)
-        quantize(w1_w[0, 0], w1_s[0, 0], w1_bf[0, 0], 0, KP)
+        quantize_w1(0, 0, 0, PACK)
         gather(v_w[1], tab_w[1], offs_sb, U32, 0, S)
         for c in range(2):
             for t in range(PACK):
@@ -248,24 +256,23 @@ def tile_list_registration_pair_features_kernel(
         cast_w1(0, 1, 0, 2, True)
         cast_w1(0, 1, 2, PACK, False)
         for t in range(0, PACK, 2):
-            quantize(w1_w[0, 1], w1_s[0, 1], w1_bf[0, 1], P * t, P * (t + 2))
+            quantize_w1(0, 1, t, t + 2)
         for c in range(2):
             for t in range(PACK):
                 mm_w1(0, 1, c, t, False, True)
-        for j0 in (0, HALF):
+        for c in range(2):
             for t in range(PACK):
-                evac_h(0, 0, t, j0, j0 + HALF)
-        for t in range(PACK):
-            evac_h(0, 1, t)
+                evac_h(0, c, t)
 
         cast_w1(1, 0, 0, PACK, True)
-        quantize(w1_w[1, 0], w1_s[1, 0], w1_bf[1, 0], 0, KP)
+        quantize_w1(1, 0, 0, PACK)
         interleave_h(0, 0, HALF, tag="w1_raw10")
         quantize_h(0, 0, HALF)
-        cast_w1(1, 1, 0, PACK, True)
+        cast_w1(1, 1, 0, 2, True)
+        cast_w1(1, 1, 2, PACK, True)
         for t in range(0, PACK, 2):
-            quantize(w1_w[1, 1], w1_s[1, 1], w1_bf[1, 1], P * t, P * (t + 2))
-        interleave_h(0, HALF, NJ, tag="w1_raw11")
+            quantize_w1(1, 1, t, t + 2)
+        interleave_h(0, HALF, NJ, tag="w1_bf110")
         quantize_h(0, HALF, NJ)
         for t in range(PACK):
             mm_w2(1, 0, t, True, False)
@@ -278,20 +285,20 @@ def tile_list_registration_pair_features_kernel(
             mm_w1(1, 0, 1, t, False, False)
             mm_w2(1, 1, t, False, True)
         cast_w3(0, 0, N, True)
-        cast_w3(1, 0, N // 2, False)
-        cast_w3(1, N // 2, N, True)
+        cast_w3(1, 0, N // 4, False)
+        cast_w3(1, N // 4, N, True)
         interleave_h(1, 0, NJ)
         quantize(w3_w[0], w3_s[0], w3_bf[0], 0, N)
         quantize(w3_w[1], w3_s[1], w3_bf[1], 0, N)
         quantize_h(1, 0, NJ)
-        interleave_h(0, 512, 768, tag="h_bf1_0")
+        interleave_h(0, 512, 768, tag="w3_bf1")
         for t in range(PACK):
             evac_h(1, 1, t)
         for u in range(N // P):
             mm_w3(0, 0, u)
         for u in range(N // P):
             mm_w3(1, 0, u)
-            finish(0, u, u == 0)
+            finish(0, u, False)
             store(0, u, u + 1)
         interleave_h(1, 512, 768)
         quantize_h(0, 512, 768)

@@ -20,7 +20,8 @@ P = 128
 PACK = 4
 KP = P * PACK
 NJ = 512
-OUT_CHUNKS = [(0, 512), (512, 768), (768, 1024)]
+OUT_CHUNKS = [(0, 256), (256, 512), (512, 768), (768, 1024)]
+OUT_BANKS = [0, 0, 1, 0]
 
 
 def tile_list_registration_pair_features_kernel(
@@ -54,8 +55,8 @@ def tile_list_registration_pair_features_kernel(
         w1_bf = {}
         w1_w = {(b, a): sb(f"w1_w{b}{a}", [P, KP], U32) for b in range(2) for a in range(2)}
         w1_s = {(b, a): sb(f"w1_s{b}{a}", [P, KP], U8) for b in range(2) for a in range(2)}
-        w3_raw = [sb(f"w3_raw{b}", [P, PACK, N], F32) for b in range(2)]
-        w3_bf = [sb(f"w3_bf{b}", [P, N * PACK], BF16) for b in range(2)]
+        w3_raw = {}
+        w3_bf = {}
         w3_w = [sb(f"w3_w{b}", [P, N], U32) for b in range(2)]
         w3_s = [sb(f"w3_s{b}", [P, N], U8) for b in range(2)]
         h_rows = {(b, c): sb(f"h_rows{b}{c}", [P, PACK, NJ], BF16) for b in range(2) for c in range(2)}
@@ -72,9 +73,10 @@ def tile_list_registration_pair_features_kernel(
             rows = w1[KP * a : KP * (a + 1), KP * b : KP * (b + 1)]
             nc.sync.dma_start(out=w1_raw[b, a][:], in_=rows.rearrange("(p j) c -> p j c", j=PACK))
 
-        def load_w3(b):
-            rows = w3[KP * b : KP * (b + 1), :]
-            nc.sync.dma_start(out=w3_raw[b][:], in_=rows.rearrange("(p j) c -> p j c", j=PACK))
+        def load_w3(b, c0, c1):
+            w3_raw[b, c0] = sb(f"w3_raw{b}_{c0}", [P, PACK, c1 - c0], F32)
+            rows = w3[KP * b : KP * (b + 1), c0:c1]
+            nc.sync.dma_start(out=w3_raw[b, c0][:], in_=rows.rearrange("(p j) c -> p j c", j=PACK))
 
         def load_words(dst, src):
             nc.sync.dma_start(out=dst, in_=src.rearrange("p n i -> p (n i)").bitcast(I32))
@@ -101,10 +103,8 @@ def tile_list_registration_pair_features_kernel(
             else:
                 nc.scalar.copy(out=dst, in_=src)
 
-        def quantize(words, scales, src, c0, c1):
-            nc.vector.quantize_mx(
-                out=words[:, c0:c1].bitcast(FP8X4), scales=scales[:, c0:c1], in_=src[:, PACK * c0 : PACK * c1]
-            )
+        def quantize_w3(b, c0, c1):
+            nc.vector.quantize_mx(out=w3_w[b][:, c0:c1].bitcast(FP8X4), scales=w3_s[b][:, c0:c1], in_=w3_bf[b, c0][:])
 
         def quantize_w1(b, a, t0, t1):
             nc.vector.quantize_mx(
@@ -138,7 +138,7 @@ def tile_list_registration_pair_features_kernel(
 
         def out_acc(d, u):
             c0, c1 = OUT_CHUNKS[d]
-            return banks[d % 2, u][:, : c1 - c0]
+            return banks[OUT_BANKS[d], u][:, c0 % NJ : c0 % NJ + c1 - c0]
 
         def mm_w3(b, d, u):
             c0, c1 = OUT_CHUNKS[d]
@@ -161,8 +161,12 @@ def tile_list_registration_pair_features_kernel(
                 scale=-1.0,
             )
 
-        def cast_w3(b, c0, c1, on_vector):
-            interleave(w3_bf[b][:, PACK * c0 : PACK * c1], w3_raw[b][:, :, c0:c1], on_vector)
+        def stage_w3(b, c0, c1):
+            w3_bf[b, c0] = sb(f"w3_bf{b}_{c0}", [P, (c1 - c0) * PACK], BF16)
+
+        def cast_w3(b, first, c0, c1, on_vector):
+            dst = w3_bf[b, first][:, PACK * (c0 - first) : PACK * (c1 - first)]
+            interleave(dst, w3_raw[b, first][:, :, c0 - first : c1 - first], on_vector)
 
         def interleave_h(b, c0, c1, tag=None):
             c = c0 // NJ
@@ -203,7 +207,7 @@ def tile_list_registration_pair_features_kernel(
                     in_=src[:].bitcast(I32)[p0 : p0 + 12 * src_step + 1 : 4 * src_step, :],
                 )
 
-        nc.gpsimd.memset(tab_s[:], 0)
+        nc.gpsimd.memset(tab_s[0:96, :], 0)
         nc.vector.memset(tab2_s[:], 0)
         nc.gpsimd.memset(w2_raw_s[:], 0)
         for a in range(2):
@@ -212,7 +216,7 @@ def tile_list_registration_pair_features_kernel(
 
         nc.sync.dma_start(out=w2_raw_w[:], in_=w2_words[0].bitcast(I32))
         nc.sync.dma_start(offs_sb[:], offs)
-        nc.sync.dma_start(out=tab_s[0:P:4, :], in_=tab_scales.rearrange("a q t -> (a q) t").bitcast(I32))
+        nc.sync.dma_start(out=tab_s[96:P, :], in_=tab_scales.rearrange("a q t -> (a q) t").bitcast(I32))
         load_words(tab_w[0][:], tab_words[0])
         nc.sync.dma_start(offs2_sb[:], offs2)
         nc.sync.dma_start(out=tab2_s[0:P:8, :], in_=tab2_scales[0].bitcast(I32))
@@ -225,16 +229,17 @@ def tile_list_registration_pair_features_kernel(
         )
         gather(v_rows, tab_s, offs_sb, U8, 0, S)
         gather(v2_rows, tab2_s, offs2_sb, U8, 0, S)
-        move_scale_rows(v_s[0], 4, v_rows, 0, 4)
+        move_scale_rows(v_s[0], 4, v_rows, 96, 1)
         load_words(tab2_w[:], tab2_words[0])
         move_scale_rows(v2_s, 0, v2_rows, 0, 8)
         load_w1(0, 1)
-        move_scale_rows(v_s[1], 8, v_rows, 64, 4)
+        move_scale_rows(v_s[1], 8, v_rows, 112, 1)
         nc.sync.dma_start(out=b1_sb[:], in_=b1.rearrange("(b p t) -> p b t", b=2, t=PACK))
         load_w1(1, 0)
         load_w1(1, 1)
-        load_w3(0)
-        load_w3(1)
+        load_w3(0, 0, N)
+        load_w3(1, 0, 256)
+        load_w3(1, 256, N)
         with nc.allow_non_contiguous_dma(reason="one bias value a partition"):
             nc.sync.dma_start(out=b3_sb[:], in_=b3.rearrange("(u p) -> p u", p=P))
 
@@ -266,14 +271,12 @@ def tile_list_registration_pair_features_kernel(
 
         cast_w1(1, 0, 0, PACK, True)
         quantize_w1(1, 0, 0, PACK)
-        interleave_h(0, 0, HALF, tag="w1_raw10")
-        quantize_h(0, 0, HALF)
+        interleave_h(0, 0, 256, tag="w1_raw10")
         cast_w1(1, 1, 0, 2, True)
         cast_w1(1, 1, 2, PACK, True)
         for t in range(0, PACK, 2):
             quantize_w1(1, 1, t, t + 2)
-        interleave_h(0, HALF, NJ, tag="w1_bf110")
-        quantize_h(0, HALF, NJ)
+        quantize_h(0, 0, 256)
         for t in range(PACK):
             mm_w2(1, 0, t, True, False)
             mm_w1(1, 0, 0, t, False, False)
@@ -284,35 +287,49 @@ def tile_list_registration_pair_features_kernel(
             mm_w1(1, 1, 1, t, True, False)
             mm_w1(1, 0, 1, t, False, False)
             mm_w2(1, 1, t, False, True)
-        cast_w3(0, 0, N, True)
-        cast_w3(1, 0, N // 4, False)
-        cast_w3(1, N // 4, N, True)
-        interleave_h(1, 0, NJ)
-        quantize(w3_w[0], w3_s[0], w3_bf[0], 0, N)
-        quantize(w3_w[1], w3_s[1], w3_bf[1], 0, N)
-        quantize_h(1, 0, NJ)
-        interleave_h(0, 512, 768, tag="w3_bf1")
-        for t in range(PACK):
+        stage_w3(0, 0, N)
+        cast_w3(0, 0, 0, N, True)
+        stage_w3(1, 0, 256)
+        stage_w3(1, 256, N)
+        cast_w3(1, 0, 0, 256, True)
+        quantize_w3(0, 0, N)
+        quantize_w3(1, 0, 256)
+        cast_w3(1, 256, 256, 384, False)
+        interleave_h(1, 0, 256, tag="w3_raw1_0")
+        cast_w3(1, 256, 384, N, True)
+        quantize_h(1, 0, 256)
+        interleave_h(0, 256, 512, tag="w3_bf1_0")
+        quantize_w3(1, 256, N)
+        for t in range(2):
             evac_h(1, 1, t)
-        for u in range(N // P):
-            mm_w3(0, 0, u)
-        for u in range(N // P):
-            mm_w3(1, 0, u)
+        for u in range(2):
+            for b in range(2):
+                mm_w3(b, 0, u)
             finish(0, u, False)
-            store(0, u, u + 1)
+        store(0, 0, 2)
+        for t in range(2, PACK):
+            evac_h(1, 1, t)
+        for u in range(2, 4):
+            for b in range(2):
+                mm_w3(b, 0, u)
+            finish(0, u, False)
+        store(0, 2, 4)
+        interleave_h(1, 256, 512)
+        quantize_h(0, 256, 512)
+        interleave_h(0, 512, 768, tag="w3_raw1_0")
+        quantize_h(1, 256, 512)
         interleave_h(1, 512, 768)
         quantize_h(0, 512, 768)
-        interleave_h(0, 768, 1024, tag="h_bf1_0")
+        interleave_h(0, 768, 1024, tag="w3_bf1_0")
         quantize_h(1, 512, 768)
         interleave_h(1, 768, 1024)
         quantize_h(0, 768, 1024)
         quantize_h(1, 768, 1024)
-        for d in (1, 2):
+        for d in (1, 2, 3):
             for b in range(2):
                 for u in range(N // P):
                     mm_w3(b, d, u)
-        for d in (1, 2):
             for u in range(N // P):
-                finish(d, u, d == 2 and u % 2 == 1)
+                finish(d, u, d == 3 and u % 2 == 1)
                 if u % 2 == 1:
                     store(d, u - 1, u + 1)

@@ -51,7 +51,12 @@ def tile_list_registration_pair_features_kernel(
         v2_s = sb("v2_s", [P, S], U8)
         v_rows = sb("v_rows", [P, S], U8)
         v2_rows = sb("v2_rows", [P, S], U8)
-        w1_raw = {(b, a): sb(f"w1_raw{b}{a}", [P, PACK, KP], F32) for b in range(2) for a in range(2)}
+        w1_raw = {(0, 0): sb("w1_raw00", [P, PACK, KP], F32)}
+        w1_half = {
+            (b, a, e): sb(f"w1_half{b}{a}{e}", [P, PACK, KP // 2], F32)
+            for b, a in ((0, 1), (1, 0), (1, 1))
+            for e in range(2)
+        }
         w1_bf = {}
         w1_w = {(b, a): sb(f"w1_w{b}{a}", [P, KP], U32) for b in range(2) for a in range(2)}
         w1_s = {(b, a): sb(f"w1_s{b}{a}", [P, KP], U8) for b in range(2) for a in range(2)}
@@ -72,6 +77,11 @@ def tile_list_registration_pair_features_kernel(
         def load_w1(b, a):
             rows = w1[KP * a : KP * (a + 1), KP * b : KP * (b + 1)]
             nc.sync.dma_start(out=w1_raw[b, a][:], in_=rows.rearrange("(p j) c -> p j c", j=PACK))
+
+        def load_w1_half(b, a, e):
+            c0 = KP * b + e * KP // 2
+            rows = w1[KP * a : KP * (a + 1), c0 : c0 + KP // 2]
+            nc.sync.dma_start(out=w1_half[b, a, e][:], in_=rows.rearrange("(p j) c -> p j c", j=PACK))
 
         def load_w3(b, c0, c1):
             w3_raw[b, c0] = sb(f"w3_raw{b}_{c0}", [P, PACK, c1 - c0], F32)
@@ -94,6 +104,23 @@ def tile_list_registration_pair_features_kernel(
                 nc.vector.tensor_scalar(out=dst, in0=src, scalar1=-1.0, scalar2=None, op0=ALU.mult)
             else:
                 nc.scalar.activation(out=dst, in_=src, func=ACT.Copy, scale=-1.0)
+
+        def cast_w1_half(b, a, e, on_vector=True):
+            if e == 0:
+                w1_bf[b, a, 0] = sb(f"w1_bf{b}{a}0", [P, PACK * KP], BF16)
+            dst = w1_bf[b, a, 0][:].rearrange("p (t m j) -> p m j t", t=PACK, j=PACK)[:, 64 * e : 64 * (e + 1), :, :]
+            src = w1_half[b, a, e][:].rearrange("p j (m t) -> p m j t", t=PACK)
+            if on_vector:
+                nc.vector.tensor_scalar(out=dst, in0=src, scalar1=-1.0, scalar2=None, op0=ALU.mult)
+            else:
+                nc.scalar.activation(out=dst, in_=src, func=ACT.Copy, scale=-1.0)
+
+        def quantize_w1_late(b, a, t0, t1):
+            nc.vector.quantize_mx(
+                out=w1_w[b, a][:, P * t0 : P * t1].bitcast(FP8X4),
+                scales=w1_s[b, a][:, P * t0 : P * t1],
+                in_=w1_bf[b, a, 0][:, KP * t0 : KP * t1],
+            )
 
         def interleave(dst, src, on_vector):
             dst = dst.rearrange("p (c i t) -> p c t i", i=4, t=PACK)
@@ -232,11 +259,13 @@ def tile_list_registration_pair_features_kernel(
         move_scale_rows(v_s[0], 4, v_rows, 96, 1)
         load_words(tab2_w[:], tab2_words[0])
         move_scale_rows(v2_s, 0, v2_rows, 0, 8)
-        load_w1(0, 1)
+        load_w1_half(0, 1, 0)
+        load_w1_half(0, 1, 1)
         move_scale_rows(v_s[1], 8, v_rows, 112, 1)
         nc.sync.dma_start(out=b1_sb[:], in_=b1.rearrange("(b p t) -> p b t", b=2, t=PACK))
-        load_w1(1, 0)
-        load_w1(1, 1)
+        for a in range(2):
+            for e in range(2):
+                load_w1_half(1, a, e)
         load_w3(0, 0, N)
         load_w3(1, 0, 256)
         load_w3(1, 256, N)
@@ -258,10 +287,10 @@ def tile_list_registration_pair_features_kernel(
             gather(v2_w, tab2_w, offs2_sb, U32, NJ * c, NJ * (c + 1))
             for t in range(PACK):
                 mm_w2(0, c, t, False, False)
-        cast_w1(0, 1, 0, 2, True)
-        cast_w1(0, 1, 2, PACK, False)
+        cast_w1_half(0, 1, 0, False)
+        cast_w1_half(0, 1, 1)
         for t in range(0, PACK, 2):
-            quantize_w1(0, 1, t, t + 2)
+            quantize_w1_late(0, 1, t, t + 2)
         for c in range(2):
             for t in range(PACK):
                 mm_w1(0, 1, c, t, False, True)
@@ -269,14 +298,17 @@ def tile_list_registration_pair_features_kernel(
             for t in range(PACK):
                 evac_h(0, c, t)
 
-        cast_w1(1, 0, 0, PACK, True)
-        quantize_w1(1, 0, 0, PACK)
-        interleave_h(0, 0, 256, tag="w1_raw10")
-        cast_w1(1, 1, 0, 2, True)
-        cast_w1(1, 1, 2, PACK, True)
+        cast_w1_half(1, 0, 0)
+        cast_w1_half(1, 0, 1)
+        quantize_w1_late(1, 0, 0, PACK)
+        cast_w1_half(1, 1, 0)
+        interleave_h(0, 0, 256, tag="w1_half110")
+        cast_w1_half(1, 1, 1)
+        interleave_h(0, 256, 512, tag="w1_half111")
         for t in range(0, PACK, 2):
-            quantize_w1(1, 1, t, t + 2)
+            quantize_w1_late(1, 1, t, t + 2)
         quantize_h(0, 0, 256)
+        quantize_h(0, 256, 512)
         for t in range(PACK):
             mm_w2(1, 0, t, True, False)
             mm_w1(1, 0, 0, t, False, False)
@@ -298,7 +330,7 @@ def tile_list_registration_pair_features_kernel(
         interleave_h(1, 0, 256, tag="w3_raw1_0")
         cast_w3(1, 256, 384, N, True)
         quantize_h(1, 0, 256)
-        interleave_h(0, 256, 512, tag="w3_bf1_0")
+        interleave_h(1, 256, 512)
         quantize_w3(1, 256, N)
         for t in range(2):
             evac_h(1, 1, t)
@@ -314,13 +346,11 @@ def tile_list_registration_pair_features_kernel(
                 mm_w3(b, 0, u)
             finish(0, u, False)
         store(0, 2, 4)
-        interleave_h(1, 256, 512)
-        quantize_h(0, 256, 512)
         interleave_h(0, 512, 768, tag="w3_raw1_0")
         quantize_h(1, 256, 512)
         interleave_h(1, 512, 768)
         quantize_h(0, 512, 768)
-        interleave_h(0, 768, 1024, tag="w3_bf1_0")
+        interleave_h(0, 768, 1024, tag="h_bf1_256")
         quantize_h(1, 512, 768)
         interleave_h(1, 768, 1024)
         quantize_h(0, 768, 1024)

@@ -302,9 +302,9 @@ def tile_list_registration_pair_features_kernel(
         cast_w1_half(1, 0, 1)
         quantize_w1_late(1, 0, 0, PACK)
         cast_w1_half(1, 1, 0)
-        interleave_h(0, 0, 256, tag="w1_half110")
+        interleave_h(0, 0, 256, tag="w1_half101")
         cast_w1_half(1, 1, 1)
-        interleave_h(0, 256, 512, tag="w1_half111")
+        interleave_h(0, 256, 512, tag="w1_half110")
         for t in range(0, PACK, 2):
             quantize_w1_late(1, 1, t, t + 2)
         quantize_h(0, 0, 256)

@@ -234,7 +234,7 @@ def tile_list_registration_pair_features_kernel(
                     in_=src[:].bitcast(I32)[p0 : p0 + 12 * src_step + 1 : 4 * src_step, :],
                 )
 
-        nc.gpsimd.memset(tab_s[0:96, :], 0)
+        nc.gpsimd.memset(tab_s[:], 0)
         nc.vector.memset(tab2_s[:], 0)
         nc.gpsimd.memset(w2_raw_s[:], 0)
         for a in range(2):
@@ -243,10 +243,10 @@ def tile_list_registration_pair_features_kernel(
 
         nc.sync.dma_start(out=w2_raw_w[:], in_=w2_words[0].bitcast(I32))
         nc.sync.dma_start(offs_sb[:], offs)
-        nc.sync.dma_start(out=tab_s[96:P, :], in_=tab_scales.rearrange("a q t -> (a q) t").bitcast(I32))
-        load_words(tab_w[0][:], tab_words[0])
         nc.sync.dma_start(offs2_sb[:], offs2)
-        nc.sync.dma_start(out=tab2_s[0:P:8, :], in_=tab2_scales[0].bitcast(I32))
+        nc.sync.dma_start(out=tab_s[0:P:4, :], in_=tab_scales.rearrange("a q t -> (a q) t").bitcast(I32))
+        load_words(tab_w[0][:], tab_words[0])
+        nc.sync.dma_start(out=tab2_s[32:96:4, :], in_=tab2_scales[0].bitcast(I32))
         load_w1(0, 0)
         load_scale_rows(w2_raw_s, w2_scales[0], 0)
         load_words(tab_w[1][:], tab_words[1])
@@ -256,12 +256,12 @@ def tile_list_registration_pair_features_kernel(
         )
         gather(v_rows, tab_s, offs_sb, U8, 0, S)
         gather(v2_rows, tab2_s, offs2_sb, U8, 0, S)
-        move_scale_rows(v_s[0], 4, v_rows, 96, 1)
+        move_scale_rows(v_s[0], 4, v_rows, 0, 4)
         load_words(tab2_w[:], tab2_words[0])
-        move_scale_rows(v2_s, 0, v2_rows, 0, 8)
+        move_scale_rows(v2_s, 0, v2_rows, 32, 4)
         load_w1_half(0, 1, 0)
         load_w1_half(0, 1, 1)
-        move_scale_rows(v_s[1], 8, v_rows, 112, 1)
+        move_scale_rows(v_s[1], 8, v_rows, 64, 4)
         nc.sync.dma_start(out=b1_sb[:], in_=b1.rearrange("(b p t) -> p b t", b=2, t=PACK))
         for a in range(2):
             for e in range(2):

from contextlib import ExitStack

import concourse.mybir as mybir

K, K2, T, T2, S, H, N = 1024, 512, 2048, 4096, 1024, 1024, 512
FLOPS = 2 * S * (K * H + K2 * H + H * N)

F32 = mybir.dt.float32
BF16 = mybir.dt.bfloat16
I32 = mybir.dt.int32
U32 = mybir.dt.uint32
U16 = mybir.dt.uint16
U8 = mybir.dt.uint8
FP8X4 = mybir.dt.float8_e4m3fn_x4
FP4X4 = mybir.dt.float4_e2m1fn_x4
ACT = mybir.ActivationFunctionType
ALU = mybir.AluOpType

P = 128
PACK = 4
KP = P * PACK
NJ = 512
OUT_CHUNKS = [(0, 256), (256, 512), (512, 768), (768, 1024)]
OUT_BANKS = [0, 0, 1, 0]


def tile_list_registration_pair_features_kernel(
    tc, tab_words, tab_scales, tab2_words, tab2_scales, offs, offs2, w1, w2_words, w2_scales, b1, w3, b3, out
):
    nc = tc.nc
    with ExitStack() as ctx:
        keep = ctx.enter_context(tc.tile_pool(name="keep", bufs=1))
        psum = ctx.enter_context(tc.psum_pool(name="psum", bufs=1))

        def sb(name, shape, dtype, tag=None):
            return keep.tile(shape, dtype, name=name, tag=tag or name, align_bytes=64)

        offs_sb = keep.tile([P, S // 16], U16, name="offs_sb")
        offs2_sb = keep.tile([P, S // 16], U16, name="offs2_sb")
        tab_w = [sb(f"tab_w{a}", [P, T], I32) for a in range(2)]
        tab2_w = sb("tab2_w", [P, T2], I32)
        tab_s = sb("tab_s", [P, T // 4], I32)
        tab2_s = sb("tab2_s", [P, T2 // 4], I32)
        w2_raw_w = sb("w2_raw_w", [P, H // 2], I32)
        w2_raw_s = sb("w2_raw_s", [P, H // 4], I32)
        w2_w = sb("w2_w", [P, 2 * H], U8)
        w2_s = sb("w2_s", [P, H], U8)
        v_w = [sb(f"v_w{a}", [P, S], U32) for a in range(2)]
        v_s = [sb(f"v_s{a}", [P, S], U8) for a in range(2)]
        v2_w = sb("v2_w", [P, S], U32)
        v2_s = sb("v2_s", [P, S], U8)
        v_rows = sb("v_rows", [P, S], U8)
        v2_rows = sb("v2_rows", [P, S], U8)
        w1_raw = {(0, 0): sb("w1_raw00", [P, PACK, KP], F32)}
        w1_half = {
            (b, a, e): sb(f"w1_half{b}{a}{e}", [P, PACK, KP // 2], F32)
            for b, a in ((0, 1), (1, 0), (1, 1))
            for e in range(2)
        }
        w1_bf = {}
        w1_w = {(b, a): sb(f"w1_w{b}{a}", [P, KP], U32) for b in range(2) for a in range(2)}
        w1_s = {(b, a): sb(f"w1_s{b}{a}", [P, KP], U8) for b in range(2) for a in range(2)}
        w3_raw = {}
        w3_bf = {}
        w3_w = [sb(f"w3_w{b}", [P, N], U32) for b in range(2)]
        w3_s = [sb(f"w3_s{b}", [P, N], U8) for b in range(2)]
        h_rows = {(b, c): sb(f"h_rows{b}{c}", [P, PACK, NJ], BF16) for b in range(2) for c in range(2)}
        h_bf = {}
        HALF = NJ // 2
        h_w = [sb(f"h_w{b}", [P, S], U32) for b in range(2)]
        h_s = [sb(f"h_s{b}", [P, S], U8) for b in range(2)]
        b1_sb = sb("b1_sb", [P, 2, PACK], F32)
        b3_sb = sb("b3_sb", [P, N // P], F32)
        res = [sb(f"res{d}", [P, N // P, c1 - c0], F32) for d, (c0, c1) in enumerate(OUT_CHUNKS)]
        banks = {(c, t): psum.tile([P, NJ], F32, name=f"bank{c}{t}") for c in range(2) for t in range(PACK)}

        def load_w1(b, a):
            rows = w1[KP * a : KP * (a + 1), KP * b : KP * (b + 1)]
            nc.sync.dma_start(out=w1_raw[b, a][:], in_=rows.rearrange("(p j) c -> p j c", j=PACK))

        def load_w1_half(b, a, e):
            c0 = KP * b + e * KP // 2
            rows = w1[KP * a : KP * (a + 1), c0 : c0 + KP // 2]
            nc.sync.dma_start(out=w1_half[b, a, e][:], in_=rows.rearrange("(p j) c -> p j c", j=PACK))

        def load_w3(b, c0, c1):
            w3_raw[b, c0] = sb(f"w3_raw{b}_{c0}", [P, PACK, c1 - c0], F32)
            rows = w3[KP * b : KP * (b + 1), c0:c1]
            nc.sync.dma_start(out=w3_raw[b, c0][:], in_=rows.rearrange("(p j) c -> p j c", j=PACK))

        def load_words(dst, src):
            nc.sync.dma_start(out=dst, in_=src.rearrange("p n i -> p (n i)").bitcast(I32))

        def gather(dst, window, offsets, dtype, c0, c1):
            nc.vector.tensor_copy(
                out=dst[:, c0:c1], in_=window[:].bitcast(dtype).indirect(offsets[:, c0 // 16 : c1 // 16])
            )

        def cast_w1(b, a, t0, t1, on_vector):
            w1_bf[b, a, t0] = sb(f"w1_bf{b}{a}{t0}", [P, (t1 - t0) * KP], BF16)
            dst = w1_bf[b, a, t0][:].rearrange("p (t m j) -> p m j t", t=t1 - t0, j=PACK)
            src = w1_raw[b, a][:].rearrange("p j (m t) -> p m j t", t=PACK)[:, :, :, t0:t1]
            if on_vector:
                nc.vector.tensor_scalar(out=dst, in0=src, scalar1=-1.0, scalar2=None, op0=ALU.mult)
            else:
                nc.scalar.activation(out=dst, in_=src, func=ACT.Copy, scale=-1.0)

        def cast_w1_half(b, a, e, on_vector=True):
            if e == 0:
                w1_bf[b, a, 0] = sb(f"w1_bf{b}{a}0", [P, PACK * KP], BF16)
            dst = w1_bf[b, a, 0][:].rearrange("p (t m j) -> p m j t", t=PACK, j=PACK)[:, 64 * e : 64 * (e + 1), :, :]
            src = w1_half[b, a, e][:].rearrange("p j (m t) -> p m j t", t=PACK)
            if on_vector:
                nc.vector.tensor_scalar(out=dst, in0=src, scalar1=-1.0, scalar2=None, op0=ALU.mult)
            else:
                nc.scalar.activation(out=dst, in_=src, func=ACT.Copy, scale=-1.0)

        def quantize_w1_late(b, a, t0, t1):
            nc.vector.quantize_mx(
                out=w1_w[b, a][:, P * t0 : P * t1].bitcast(FP8X4),
                scales=w1_s[b, a][:, P * t0 : P * t1],
                in_=w1_bf[b, a, 0][:, KP * t0 : KP * t1],
            )

        def interleave(dst, src, on_vector):
            dst = dst.rearrange("p (c i t) -> p c t i", i=4, t=PACK)
            src = src.rearrange("p t (c i) -> p c t i", i=4)
            if on_vector:
                nc.vector.tensor_copy(out=dst, in_=src)
            else:
                nc.scalar.copy(out=dst, in_=src)

        def quantize_w3(b, c0, c1):
            nc.vector.quantize_mx(out=w3_w[b][:, c0:c1].bitcast(FP8X4), scales=w3_s[b][:, c0:c1], in_=w3_bf[b, c0][:])

        def quantize_w1(b, a, t0, t1):
            nc.vector.quantize_mx(
                out=w1_w[b, a][:, P * t0 : P * t1].bitcast(FP8X4),
                scales=w1_s[b, a][:, P * t0 : P * t1],
                in_=w1_bf[b, a, t0][:],
            )

        def mm_w2(b, c, t, start, stop):
            r0 = KP * b + P * t
            nc.tensor.matmul_mx(
                out=banks[c, t][:],
                lhsT=w2_w[:, 2 * r0 : 2 * (r0 + P)].bitcast(FP4X4),
                lhsT_scale=w2_s[:, r0 : r0 + P],
                rhs=v2_w[:, NJ * c : NJ * (c + 1)].bitcast(FP8X4),
                rhs_scale=v2_s[:, NJ * c : NJ * (c + 1)],
                start=start,
                stop=stop,
            )

        def mm_w1(b, a, c, t, start, stop):
            nc.tensor.matmul_mx(
                out=banks[c, t][:],
                lhsT=w1_w[b, a][:, P * t : P * (t + 1)].bitcast(FP8X4),
                lhsT_scale=w1_s[b, a][:, P * t : P * (t + 1)],
                rhs=v_w[a][:, NJ * c : NJ * (c + 1)].bitcast(FP8X4),
                rhs_scale=v_s[a][4 * (a + 1) :, NJ * c : NJ * (c + 1)],
                start=start,
                stop=stop,
            )

        def out_acc(d, u):
            c0, c1 = OUT_CHUNKS[d]
            return banks[OUT_BANKS[d], u][:, c0 % NJ : c0 % NJ + c1 - c0]

        def mm_w3(b, d, u):
            c0, c1 = OUT_CHUNKS[d]
            nc.tensor.matmul_mx(
                out=out_acc(d, u),
                lhsT=w3_w[b][:, P * u : P * (u + 1)].bitcast(FP8X4),
                lhsT_scale=w3_s[b][:, P * u : P * (u + 1)],
                rhs=h_w[b][:, c0:c1].bitcast(FP8X4),
                rhs_scale=h_s[b][:, c0:c1],
                start=(b == 0),
                stop=(b == 1),
            )

        def evac_h(b, c, t, j0=0, j1=NJ):
            nc.scalar.activation(
                out=h_rows[b, c][:, t, j0:j1],
                in_=banks[c, t][:, j0:j1],
                func=ACT.Abs,
                bias=b1_sb[:, b, t : t + 1],
                scale=-1.0,
            )

        def stage_w3(b, c0, c1):
            w3_bf[b, c0] = sb(f"w3_bf{b}_{c0}", [P, (c1 - c0) * PACK], BF16)

        def cast_w3(b, first, c0, c1, on_vector):
            dst = w3_bf[b, first][:, PACK * (c0 - first) : PACK * (c1 - first)]
            interleave(dst, w3_raw[b, first][:, :, c0 - first : c1 - first], on_vector)

        def interleave_h(b, c0, c1, tag=None):
            c = c0 // NJ
            h_bf[b, c0] = sb(f"h_bf{b}_{c0}", [P, (c1 - c0) * PACK], BF16, tag=tag)
            interleave(h_bf[b, c0][:], h_rows[b, c][:, :, c0 - NJ * c : c1 - NJ * c], True)

        def h_src(b, c0, c1):
            first = max(f for bb, f in h_bf if bb == b and f <= c0)
            return h_bf[b, first][:, PACK * (c0 - first) : PACK * (c1 - first)]

        def quantize_h(b, c0, c1):
            nc.vector.quantize_mx(out=h_w[b][:, c0:c1].bitcast(FP8X4), scales=h_s[b][:, c0:c1], in_=h_src(b, c0, c1))

        def finish(d, u, on_vector):
            c0, c1 = OUT_CHUNKS[d]
            acc = out_acc(d, u)
            if on_vector:
                nc.vector.tensor_scalar(
                    out=res[d][:, u, :], in0=acc, scalar1=b3_sb[:, u : u + 1], scalar2=0.0, op0=ALU.add, op1=ALU.max
                )
            else:
                nc.scalar.activation(out=res[d][:, u, :], in_=acc, func=ACT.Relu, bias=b3_sb[:, u : u + 1])

        def store(d, u0, u1):
            c0, c1 = OUT_CHUNKS[d]
            rows = out[P * u0 : P * u1, c0:c1].rearrange("(u p) j -> p u j", p=P)
            nc.sync.dma_start(out=rows, in_=res[d][:, u0:u1, :])

        def load_scale_rows(dst, rows, first):
            for r in range(4):
                nc.sync.dma_start(out=dst[first + r : P : 32, :], in_=rows.bitcast(I32)[r : 16 : 4, :])

        def move_scale_rows(dst, first, src, src_first, src_step):
            for r in range(4):
                p0 = src_first + src_step * r
                nc.sync.dma_start(
                    out=dst[:].bitcast(I32)[first + r : P : 32, :],
                    in_=src[:].bitcast(I32)[p0 : p0 + 12 * src_step + 1 : 4 * src_step, :],
                )

        nc.gpsimd.memset(tab_s[:], 0)
        nc.vector.memset(tab2_s[:], 0)
        nc.gpsimd.memset(w2_raw_s[:], 0)
        for a in range(2):
            nc.vector.memset(v_s[a][:].bitcast(I32), 0)
        nc.vector.memset(v2_s[:].bitcast(I32), 0)

        nc.sync.dma_start(out=w2_raw_w[:], in_=w2_words[0].bitcast(I32))
        nc.sync.dma_start(offs_sb[:], offs)
        nc.sync.dma_start(offs2_sb[:], offs2)
        nc.sync.dma_start(out=tab_s[0:P:4, :], in_=tab_scales.rearrange("a q t -> (a q) t").bitcast(I32))
        load_words(tab_w[0][:], tab_words[0])
        nc.sync.dma_start(out=tab2_s[32:96:4, :], in_=tab2_scales[0].bitcast(I32))
        load_w1(0, 0)
        load_scale_rows(w2_raw_s, w2_scales[0], 0)
        load_words(tab_w[1][:], tab_words[1])
        nc.vector.tensor_copy(
            out=w2_w[:].bitcast(U16).rearrange("p (b t m) -> p b m t", b=2, t=PACK),
            in_=w2_raw_w[:].bitcast(U16).rearrange("p (b m t) -> p b m t", b=2, t=PACK),
        )
        gather(v_rows, tab_s, offs_sb, U8, 0, S)
        gather(v2_rows, tab2_s, offs2_sb, U8, 0, S)
        move_scale_rows(v_s[0], 4, v_rows, 0, 4)
        load_words(tab2_w[:], tab2_words[0])
        move_scale_rows(v2_s, 0, v2_rows, 32, 4)
        load_w1_half(0, 1, 0)
        load_w1_half(0, 1, 1)
        move_scale_rows(v_s[1], 8, v_rows, 64, 4)
        nc.sync.dma_start(out=b1_sb[:], in_=b1.rearrange("(b p t) -> p b t", b=2, t=PACK))
        for a in range(2):
            for e in range(2):
                load_w1_half(1, a, e)
        load_w3(0, 0, N)
        load_w3(1, 0, 256)
        load_w3(1, 256, N)
        with nc.allow_non_contiguous_dma(reason="one bias value a partition"):
            nc.sync.dma_start(out=b3_sb[:], in_=b3.rearrange("(u p) -> p u", p=P))

        gather(v_w[0], tab_w[0], offs_sb, U32, 0, S)
        cast_w1(0, 0, 0, PACK, False)
        quantize_w1(0, 0, 0, PACK)
        gather(v_w[1], tab_w[1], offs_sb, U32, 0, S)
        for c in range(2):
            for t in range(PACK):
                mm_w1(0, 0, c, t, True, False)
        nc.vector.tensor_copy(
            out=w2_s[:].rearrange("p (b t m) -> p b m t", b=2, t=PACK),
            in_=w2_raw_s[:].bitcast(U8).rearrange("p (b m t) -> p b m t", b=2, t=PACK),
        )
        for c in range(2):
            gather(v2_w, tab2_w, offs2_sb, U32, NJ * c, NJ * (c + 1))
            for t in range(PACK):
                mm_w2(0, c, t, False, False)
        cast_w1_half(0, 1, 0, False)
        cast_w1_half(0, 1, 1)
        for t in range(0, PACK, 2):
            quantize_w1_late(0, 1, t, t + 2)
        for c in range(2):
            for t in range(PACK):
                mm_w1(0, 1, c, t, False, True)
        for c in range(2):
            for t in range(PACK):
                evac_h(0, c, t)

        cast_w1_half(1, 0, 0)
        cast_w1_half(1, 0, 1)
        quantize_w1_late(1, 0, 0, PACK)
        cast_w1_half(1, 1, 0)
        interleave_h(0, 0, 256, tag="w1_half101")
        cast_w1_half(1, 1, 1)
        interleave_h(0, 256, 512, tag="w1_half110")
        for t in range(0, PACK, 2):
            quantize_w1_late(1, 1, t, t + 2)
        quantize_h(0, 0, 256)
        quantize_h(0, 256, 512)
        for t in range(PACK):
            mm_w2(1, 0, t, True, False)
            mm_w1(1, 0, 0, t, False, False)
        for t in range(PACK):
            mm_w1(1, 1, 0, t, False, True)
            evac_h(1, 0, t)
        for t in range(PACK):
            mm_w1(1, 1, 1, t, True, False)
            mm_w1(1, 0, 1, t, False, False)
            mm_w2(1, 1, t, False, True)
        stage_w3(0, 0, N)
        cast_w3(0, 0, 0, N, True)
        stage_w3(1, 0, 256)
        stage_w3(1, 256, N)
        cast_w3(1, 0, 0, 256, True)
        quantize_w3(0, 0, N)
        quantize_w3(1, 0, 256)
        cast_w3(1, 256, 256, 384, False)
        interleave_h(1, 0, 256, tag="w3_raw1_0")
        cast_w3(1, 256, 384, N, True)
        quantize_h(1, 0, 256)
        interleave_h(1, 256, 512)
        quantize_w3(1, 256, N)
        for t in range(2):
            evac_h(1, 1, t)
        for u in range(2):
            for b in range(2):
                mm_w3(b, 0, u)
            finish(0, u, False)
        store(0, 0, 2)
        for t in range(2, PACK):
            evac_h(1, 1, t)
        for u in range(2, 4):
            for b in range(2):
                mm_w3(b, 0, u)
            finish(0, u, False)
        store(0, 2, 4)
        interleave_h(0, 512, 768, tag="w3_raw1_0")
        quantize_h(1, 256, 512)
        interleave_h(1, 512, 768)
        quantize_h(0, 512, 768)
        interleave_h(0, 768, 1024, tag="h_bf1_256")
        quantize_h(1, 512, 768)
        interleave_h(1, 768, 1024)
        quantize_h(0, 768, 1024)
        quantize_h(1, 768, 1024)
        for d in (1, 2, 3):
            for b in range(2):
                for u in range(N // P):
                    mm_w3(b, d, u)
            for u in range(N // P):
                finish(d, u, d == 3 and u % 2 == 1)
                if u % 2 == 1:
                    store(d, u - 1, u + 1)
